import numpy as np
import ml_dtypes


def mxq(x, axis, fmt="e4m3"):
    dtype, down = {"e4m3": (ml_dtypes.float8_e4m3fn, 7), "e5m2": (ml_dtypes.float8_e5m2, 14)}[fmt]
    v = np.moveaxis(np.asarray(x, np.float32).astype(ml_dtypes.bfloat16).astype(np.float64), axis, -1)
    blocks = v.reshape(v.shape[:-1] + (-1, 32))
    amax = np.abs(blocks).max(-1, keepdims=True)
    byte = np.maximum(np.where(amax > 0, np.frexp(amax)[1] - 1 + 127, 0) - down, 1)
    scale = np.exp2(byte - 127.0)
    codes = (blocks / scale).astype(np.float32).astype(dtype).astype(np.float64)
    return np.moveaxis((codes * scale).reshape(v.shape), -1, axis)


WIDE = False


def mx_kscale(k):
    if not WIDE:
        return np.ones(k)
    levels = np.array([10, -10, 5, -5, 0])
    if k % 512:
        return np.exp2(np.random.permutation(np.resize(levels, k // 32))).repeat(32)
    a = np.empty((k // 512, 16))
    for p in range(k // 512):
        a[p, :8] = np.random.permutation(np.resize(levels, 8))
        for g in range(8):
            far = levels[np.abs(levels - a[p, g]) >= 10]
            a[p, g + 8] = far[np.random.randint(len(far))]
    return np.exp2(a.ravel()).repeat(32)


def f64(x):
    return np.asarray(x).astype(np.float64)


def striped(idx):
    return np.tile(idx.reshape(-1, 16).T, (8, 1)).astype(np.uint16)


def unstriped(offs):
    return offs[:16].T.reshape(-1).astype(np.int64)


def pack_weight(w):
    k, n = w.shape
    w = f64(np.asarray(w, np.float32).astype(ml_dtypes.bfloat16)).reshape(k // 32, 32, n)
    amax = np.abs(w).max(1)
    byte = np.clip(np.where(amax > 0, np.frexp(amax)[1] - 1 + 127 - 7, 1), 1, 254)
    scaled = (w * np.exp2(127.0 - byte)[:, None, :]).reshape(k, n).astype(np.float32)
    words = np.ascontiguousarray(scaled.reshape(k // 512, 128, 4, n).transpose(0, 1, 3, 2)).astype(ml_dtypes.float8_e4m3fn).view(np.uint8)
    return words, np.ascontiguousarray(byte.astype(np.uint8).reshape(k // 512, 16, n))


def unpack_weight(words, scales):
    g, p, n, _ = words.shape
    vals = np.ascontiguousarray(words).view(ml_dtypes.float8_e4m3fn).astype(np.float64) * np.repeat(np.exp2(scales.astype(np.float64) - 127.0), 8, axis=1)[..., None]
    return vals.transpose(0, 1, 3, 2).reshape(g * 512, n)


K, T, S, H, N, U = 512, 1024, 512, 512, 128, 1024


def setup_inputs():
    n = np.random.standard_normal
    s = mx_kscale(K)[:, None]
    u = mx_kscale(H)
    packed_xT = pack_weight(n((K, T)) * s)
    return {
        "x_words": packed_xT[0],
        "x_scales": packed_xT[1],
        "mem": (n((H, U)) * u[:, None]).astype(np.float32),
        "w1": (n((K, N)) / np.sqrt(2 * K) / s).astype(np.float32),
        "ar": (n((H, N)) / np.sqrt(2 * H) / u[:, None]).astype(np.float32),
        "bias": (0.5 * n((N, 1))).astype(np.float32),
        "offs": striped(np.random.permutation(T)[:S]),
        "slot": striped(np.random.permutation(U)[:S]),
    }


def reference(x_words, x_scales, mem, w1, ar, bias, offs, slot):
    h = f64(mem)[:, unstriped(slot)]
    xq = unpack_weight(x_words, x_scales)[:, unstriped(offs)]
    return np.tanh((mxq(f64(ar), 0, "e4m3").T @ mxq(h, 0, "e4m3") + mxq(f64(w1), 0, "e4m3").T @ xq) + f64(bias))

@@ -1,0 +1,96 @@
+from contextlib import ExitStack
+
+import concourse.mybir as mybir
+
+K, T, S, H, N, U = 512, 1024, 512, 512, 128, 1024
+FLOPS = 2 * (K + H) * N * S
+
+F32 = mybir.dt.float32
+BF16 = mybir.dt.bfloat16
+I32 = mybir.dt.int32
+U32 = mybir.dt.uint32
+U16 = mybir.dt.uint16
+U8 = mybir.dt.uint8
+FP8X4 = mybir.dt.float8_e4m3fn_x4
+TANH = mybir.ActivationFunctionType.Tanh
+
+P = 128
+PACK = 4
+PIECE = 128
+PIECES = S // PIECE
+
+
+def tile_picked_ylmu_rnn_p_kernel(tc, x_words, x_scales, mem, w1, ar, bias, offs, slot, out):
+    nc = tc.nc
+    with ExitStack() as ctx:
+        keep = ctx.enter_context(tc.tile_pool(name="keep", bufs=1))
+        psum = ctx.enter_context(tc.psum_pool(name="psum", bufs=1))
+
+        offs_sb = keep.tile([P, S // 16], U16, name="offs_sb")
+        slot_sb = keep.tile([P, S // 16], U16, name="slot_sb")
+        scale_table = keep.tile([P, T], U8, name="scale_table", align_bytes=64)
+        word_table = keep.tile([P, T], I32, name="word_table", align_bytes=64)
+        mem_rows = [keep.tile([P, U], F32, name="mem_rows%d" % t, align_bytes=64) for t in range(PACK)]
+        w_raw = [keep.tile([P, PACK, N], F32, name="w_raw%d" % i, align_bytes=64) for i in range(2)]
+        bias_sb = keep.tile([P, 1], F32, name="bias_sb")
+        zero = keep.tile([P, 1], F32, name="zero")
+        warm = keep.tile([P, 1], F32, name="warm")
+
+        mem_view = mem.rearrange("(p t) u -> p t u", t=PACK)
+
+        nc.vector.memset(scale_table[:].bitcast(I32), 0)
+        nc.vector.memset(zero[:], 0.0)
+        nc.sync.dma_start(offs_sb[:], offs)
+        for q in range(4):
+            nc.scalar.dma_start(scale_table[32 * q : 32 * q + 4, :].bitcast(I32), x_scales[0, 4 * q : 4 * q + 4, :].bitcast(I32))
+        nc.sync.dma_start(slot_sb[:], slot)
+        nc.sync.dma_start(mem_rows[0][:], mem_view[:, 0, :])
+        nc.sync.dma_start(mem_rows[1][:], mem_view[:, 1, :])
+        nc.sync.dma_start(w_raw[0][:], ar.rearrange("(p t) n -> p t n", t=PACK))
+        nc.sync.dma_start(mem_rows[2][:], mem_view[:, 2, :])
+        nc.sync.dma_start(w_raw[1][:], w1.rearrange("(p t) n -> p t n", t=PACK))
+        nc.sync.dma_start(mem_rows[3][:], mem_view[:, 3, :])
+        nc.sync.dma_start(word_table[:], x_words[0].rearrange("p c r -> p (c r)").bitcast(I32))
+        nc.sync.dma_start(bias_sb[:], bias)
+
+        nc.scalar.activation(warm[:], zero[:], TANH)
+
+        x_scale = keep.tile([P, S], U8, name="x_scale", align_bytes=64)
+        nc.vector.tensor_copy(x_scale[:], scale_table[:].indirect(offs_sb[:]))
+
+        h_rows = keep.tile([P, PACK, S], BF16, name="h_rows", align_bytes=64)
+        for t in range(PACK - 1):
+            nc.vector.tensor_copy(h_rows[:, t, :], mem_rows[t][:].indirect(slot_sb[:]))
+
+        w_bf = keep.tile([P, 2, N, PACK], BF16, name="w_bf", align_bytes=64)
+        for i in range(2):
+            nc.scalar.copy(w_bf[:, i, :, :], w_raw[i][:].rearrange("p t n -> p n t"))
+        w_code = keep.tile([P, 2 * N], U32, name="w_code", align_bytes=64)
+        w_scale = keep.tile([P, 2 * N], U8, name="w_scale", align_bytes=64)
+        nc.vector.quantize_mx(out=w_code[:].bitcast(FP8X4), scales=w_scale[:], in_=w_bf[:].rearrange("p i n t -> p (i n t)"))
+
+        h_bf = []
+        for c in range(PIECES):
+            cols = slice(c * PIECE, (c + 1) * PIECE)
+            entries = slice(c * PIECE // 16, (c + 1) * PIECE // 16)
+            nc.vector.tensor_copy(h_rows[:, PACK - 1, cols], mem_rows[PACK - 1][:].indirect(slot_sb[:, entries]))
+            grouped = keep.tile([P, PIECE, PACK], BF16, name="h_bf%d" % c, align_bytes=64)
+            nc.scalar.copy(grouped[:], h_rows[:, :, cols].rearrange("p t c -> p c t"))
+            h_bf.append(grouped)
+
+        for c in range(PIECES):
+            cols = slice(c * PIECE, (c + 1) * PIECE)
+            entries = slice(c * PIECE // 16, (c + 1) * PIECE // 16)
+            x_code = keep.tile([P, PIECE], U32, name="x_code%d" % c, align_bytes=64)
+            nc.vector.tensor_copy(x_code[:], word_table[:].bitcast(U32).indirect(offs_sb[:, entries]))
+            h_code = keep.tile([P, PIECE], U32, name="h_code%d" % c, align_bytes=64)
+            h_scale = keep.tile([P, PIECE], U8, name="h_scale%d" % c, align_bytes=64)
+            nc.vector.quantize_mx(out=h_code[:].bitcast(FP8X4), scales=h_scale[:], in_=h_bf[c][:].rearrange("p c t -> p (c t)"))
+            acc = psum.tile([P, PIECE], F32, name="acc%d" % c)
+            nc.tensor.matmul_mx(out=acc[:], lhsT=w_code[:, N : 2 * N].bitcast(FP8X4), lhsT_scale=w_scale[:, N : 2 * N],
+                                rhs=x_code[:].bitcast(FP8X4), rhs_scale=x_scale[:, cols], start=True, stop=False)
+            nc.tensor.matmul_mx(out=acc[:], lhsT=w_code[:, 0:N].bitcast(FP8X4), lhsT_scale=w_scale[:, 0:N],
+                                rhs=h_code[:].bitcast(FP8X4), rhs_scale=h_scale[:], start=False, stop=True)
+            result = keep.tile([P, PIECE], F32, name="result%d" % c)
+            nc.scalar.activation(result[:], acc[:], TANH, bias=bias_sb[:])
+            nc.sync.dma_start(out[:, cols], result[:])

@@ -16,8 +16,6 @@ TANH = mybir.ActivationFunctionType.Tanh
 
 P = 128
 PACK = 4
-PIECE = 128
-PIECES = S // PIECE
 
 
 def tile_picked_ylmu_rnn_p_kernel(tc, x_words, x_scales, mem, w1, ar, bias, offs, slot, out):
@@ -31,7 +29,8 @@ def tile_picked_ylmu_rnn_p_kernel(tc, x_words, x_scales, mem, w1, ar, bias, offs
         scale_table = keep.tile([P, T], U8, name="scale_table", align_bytes=64)
         word_table = keep.tile([P, T], I32, name="word_table", align_bytes=64)
         mem_rows = [keep.tile([P, U], F32, name="mem_rows%d" % t, align_bytes=64) for t in range(PACK)]
-        w_raw = [keep.tile([P, PACK, N], F32, name="w_raw%d" % i, align_bytes=64) for i in range(2)]
+        ar_raw = keep.tile([P, PACK, N], F32, name="ar_raw", align_bytes=64)
+        w1_raw = keep.tile([P, PACK, N], F32, name="w1_raw", align_bytes=64)
         bias_sb = keep.tile([P, 1], F32, name="bias_sb")
         zero = keep.tile([P, 1], F32, name="zero")
         warm = keep.tile([P, 1], F32, name="warm")
@@ -41,14 +40,14 @@ def tile_picked_ylmu_rnn_p_kernel(tc, x_words, x_scales, mem, w1, ar, bias, offs
         nc.vector.memset(scale_table[:].bitcast(I32), 0)
         nc.vector.memset(zero[:], 0.0)
         nc.sync.dma_start(offs_sb[:], offs)
-        for q in range(4):
-            nc.scalar.dma_start(scale_table[32 * q : 32 * q + 4, :].bitcast(I32), x_scales[0, 4 * q : 4 * q + 4, :].bitcast(I32))
         nc.sync.dma_start(slot_sb[:], slot)
+        nc.sync.dma_start(ar_raw[:], ar.rearrange("(p t) n -> p t n", t=PACK))
+        for q in range(4):
+            nc.sync.dma_start(scale_table[32 * q : 32 * q + 4, :].bitcast(I32), x_scales[0, 4 * q : 4 * q + 4, :].bitcast(I32))
         nc.sync.dma_start(mem_rows[0][:], mem_view[:, 0, :])
         nc.sync.dma_start(mem_rows[1][:], mem_view[:, 1, :])
-        nc.sync.dma_start(w_raw[0][:], ar.rearrange("(p t) n -> p t n", t=PACK))
         nc.sync.dma_start(mem_rows[2][:], mem_view[:, 2, :])
-        nc.sync.dma_start(w_raw[1][:], w1.rearrange("(p t) n -> p t n", t=PACK))
+        nc.sync.dma_start(w1_raw[:], w1.rearrange("(p t) n -> p t n", t=PACK))
         nc.sync.dma_start(mem_rows[3][:], mem_view[:, 3, :])
         nc.sync.dma_start(word_table[:], x_words[0].rearrange("p c r -> p (c r)").bitcast(I32))
         nc.sync.dma_start(bias_sb[:], bias)
@@ -63,34 +62,39 @@ def tile_picked_ylmu_rnn_p_kernel(tc, x_words, x_scales, mem, w1, ar, bias, offs
             nc.vector.tensor_copy(h_rows[:, t, :], mem_rows[t][:].indirect(slot_sb[:]))
 
         w_bf = keep.tile([P, 2, N, PACK], BF16, name="w_bf", align_bytes=64)
-        for i in range(2):
-            nc.scalar.copy(w_bf[:, i, :, :], w_raw[i][:].rearrange("p t n -> p n t"))
+        for i, raw in enumerate((ar_raw, w1_raw)):
+            nc.scalar.copy(w_bf[:, i, :, :], raw[:].rearrange("p t n -> p n t"))
         w_code = keep.tile([P, 2 * N], U32, name="w_code", align_bytes=64)
         w_scale = keep.tile([P, 2 * N], U8, name="w_scale", align_bytes=64)
         nc.vector.quantize_mx(out=w_code[:].bitcast(FP8X4), scales=w_scale[:], in_=w_bf[:].rearrange("p i n t -> p (i n t)"))
 
+        for a, b in ((0, 128), (128, 256), (256, 512)):
+            nc.vector.tensor_copy(h_rows[:, PACK - 1, a:b], mem_rows[PACK - 1][:].indirect(slot_sb[:, a // 16 : b // 16]))
+        pieces = ((0, 128), (128, 256), (256, 384), (384, 512))
         h_bf = []
-        for c in range(PIECES):
-            cols = slice(c * PIECE, (c + 1) * PIECE)
-            entries = slice(c * PIECE // 16, (c + 1) * PIECE // 16)
-            nc.vector.tensor_copy(h_rows[:, PACK - 1, cols], mem_rows[PACK - 1][:].indirect(slot_sb[:, entries]))
-            grouped = keep.tile([P, PIECE, PACK], BF16, name="h_bf%d" % c, align_bytes=64)
-            nc.scalar.copy(grouped[:], h_rows[:, :, cols].rearrange("p t c -> p c t"))
+        for a, b in pieces:
+            grouped = keep.tile([P, b - a, PACK], BF16, name="h_bf%d" % a, align_bytes=64)
+            for c in range(a, b, 128):
+                nc.scalar.copy(grouped[:, c - a : c - a + 128, :], h_rows[:, :, c : c + 128].rearrange("p t c -> p c t"))
             h_bf.append(grouped)
 
-        for c in range(PIECES):
-            cols = slice(c * PIECE, (c + 1) * PIECE)
-            entries = slice(c * PIECE // 16, (c + 1) * PIECE // 16)
-            x_code = keep.tile([P, PIECE], U32, name="x_code%d" % c, align_bytes=64)
-            nc.vector.tensor_copy(x_code[:], word_table[:].bitcast(U32).indirect(offs_sb[:, entries]))
-            h_code = keep.tile([P, PIECE], U32, name="h_code%d" % c, align_bytes=64)
-            h_scale = keep.tile([P, PIECE], U8, name="h_scale%d" % c, align_bytes=64)
-            nc.vector.quantize_mx(out=h_code[:].bitcast(FP8X4), scales=h_scale[:], in_=h_bf[c][:].rearrange("p c t -> p (c t)"))
-            acc = psum.tile([P, PIECE], F32, name="acc%d" % c)
+        h_code, h_scale = [], []
+        x_code = keep.tile([P, S], U32, name="x_code", align_bytes=64)
+        for n, (a, b) in enumerate(pieces):
+            code = keep.tile([P, b - a], U32, name="h_code%d" % a, align_bytes=64)
+            scale = keep.tile([P, b - a], U8, name="h_scale%d" % a, align_bytes=64)
+            nc.vector.quantize_mx(out=code[:].bitcast(FP8X4), scales=scale[:], in_=h_bf[n][:].rearrange("p c t -> p (c t)"))
+            h_code.append(code)
+            h_scale.append(scale)
+            if n == 0:
+                for xa, xb in ((0, 256), (256, 512)):
+                    nc.vector.tensor_copy(x_code[:, xa:xb], word_table[:].bitcast(U32).indirect(offs_sb[:, xa // 16 : xb // 16]))
+        for n, (a, b) in enumerate(pieces):
+            acc = psum.tile([P, b - a], F32, name="acc%d" % a)
             nc.tensor.matmul_mx(out=acc[:], lhsT=w_code[:, N : 2 * N].bitcast(FP8X4), lhsT_scale=w_scale[:, N : 2 * N],
-                                rhs=x_code[:].bitcast(FP8X4), rhs_scale=x_scale[:, cols], start=True, stop=False)
+                                rhs=x_code[:, a:b].bitcast(FP8X4), rhs_scale=x_scale[:, a:b], start=True, stop=False)
             nc.tensor.matmul_mx(out=acc[:], lhsT=w_code[:, 0:N].bitcast(FP8X4), lhsT_scale=w_scale[:, 0:N],
-                                rhs=h_code[:].bitcast(FP8X4), rhs_scale=h_scale[:], start=False, stop=True)
-            result = keep.tile([P, PIECE], F32, name="result%d" % c)
+                                rhs=h_code[n][:].bitcast(FP8X4), rhs_scale=h_scale[n][:], start=False, stop=True)
+            result = keep.tile([P, b - a], F32, name="result%d" % a)
             nc.scalar.activation(result[:], acc[:], TANH, bias=bias_sb[:])
-            nc.sync.dma_start(out[:, cols], result[:])
+            nc.sync.dma_start(out[:, a:b], result[:])

@@ -12,10 +12,17 @@ U32 = mybir.dt.uint32
 U16 = mybir.dt.uint16
 U8 = mybir.dt.uint8
 FP8X4 = mybir.dt.float8_e4m3fn_x4
+COPY = mybir.ActivationFunctionType.Copy
 TANH = mybir.ActivationFunctionType.Tanh
 
 P = 128
 PACK = 4
+QUADRANTS = 4
+LIST_ROWS = 16
+PIECE = 128
+PIECES = S // PIECE
+LAST_PLANE_CUTS = ((0, PIECE), (PIECE, 2 * PIECE), (2 * PIECE, S))
+WORD_CUTS = ((0, 2 * PIECE), (2 * PIECE, 3 * PIECE), (3 * PIECE, S))
 
 
 def tile_picked_ylmu_rnn_p_kernel(tc, x_words, x_scales, mem, w1, ar, bias, offs, slot, out):
@@ -24,77 +31,91 @@ def tile_picked_ylmu_rnn_p_kernel(tc, x_words, x_scales, mem, w1, ar, bias, offs
         keep = ctx.enter_context(tc.tile_pool(name="keep", bufs=1))
         psum = ctx.enter_context(tc.psum_pool(name="psum", bufs=1))
 
-        offs_sb = keep.tile([P, S // 16], U16, name="offs_sb")
-        slot_sb = keep.tile([P, S // 16], U16, name="slot_sb")
+        offs_sb = keep.tile([P, S // LIST_ROWS], U16, name="offs_sb")
+        slot_sb = keep.tile([P, S // LIST_ROWS], U16, name="slot_sb")
         scale_table = keep.tile([P, T], U8, name="scale_table", align_bytes=64)
         word_table = keep.tile([P, T], I32, name="word_table", align_bytes=64)
-        mem_rows = [keep.tile([P, U], F32, name="mem_rows%d" % t, align_bytes=64) for t in range(PACK)]
+        mem_planes = [keep.tile([P, U], F32, name="mem_plane%d" % t, align_bytes=64) for t in range(PACK)]
         ar_raw = keep.tile([P, PACK, N], F32, name="ar_raw", align_bytes=64)
         w1_raw = keep.tile([P, PACK, N], F32, name="w1_raw", align_bytes=64)
         bias_sb = keep.tile([P, 1], F32, name="bias_sb")
-        zero = keep.tile([P, 1], F32, name="zero")
-        warm = keep.tile([P, 1], F32, name="warm")
 
-        mem_view = mem.rearrange("(p t) u -> p t u", t=PACK)
+        def entries(list_tile, a, b):
+            return list_tile[:, a // LIST_ROWS : b // LIST_ROWS]
 
         nc.vector.memset(scale_table[:].bitcast(I32), 0)
-        nc.vector.memset(zero[:], 0.0)
+
+        mem_view = mem.rearrange("(p t) u -> p t u", t=PACK)
         nc.sync.dma_start(offs_sb[:], offs)
         nc.sync.dma_start(slot_sb[:], slot)
         nc.sync.dma_start(ar_raw[:], ar.rearrange("(p t) n -> p t n", t=PACK))
-        for q in range(4):
-            nc.sync.dma_start(scale_table[32 * q : 32 * q + 4, :].bitcast(I32), x_scales[0, 4 * q : 4 * q + 4, :].bitcast(I32))
-        nc.sync.dma_start(mem_rows[0][:], mem_view[:, 0, :])
-        nc.sync.dma_start(mem_rows[1][:], mem_view[:, 1, :])
-        nc.sync.dma_start(mem_rows[2][:], mem_view[:, 2, :])
+        for q in range(QUADRANTS):
+            nc.sync.dma_start(
+                scale_table[32 * q : 32 * q + 4, :].bitcast(I32),
+                x_scales[0, 4 * q : 4 * q + 4, :].bitcast(I32),
+            )
+        for t in range(PACK - 1):
+            nc.sync.dma_start(mem_planes[t][:], mem_view[:, t, :])
         nc.sync.dma_start(w1_raw[:], w1.rearrange("(p t) n -> p t n", t=PACK))
-        nc.sync.dma_start(mem_rows[3][:], mem_view[:, 3, :])
-        nc.sync.dma_start(word_table[:], x_words[0].rearrange("p c r -> p (c r)").bitcast(I32))
+        nc.sync.dma_start(mem_planes[PACK - 1][:], mem_view[:, PACK - 1, :])
+        nc.sync.dma_start(word_table[:], x_words[0].rearrange("p c t -> p (c t)").bitcast(I32))
         nc.sync.dma_start(bias_sb[:], bias)
-
-        nc.scalar.activation(warm[:], zero[:], TANH)
 
         x_scale = keep.tile([P, S], U8, name="x_scale", align_bytes=64)
         nc.vector.tensor_copy(x_scale[:], scale_table[:].indirect(offs_sb[:]))
 
-        h_rows = keep.tile([P, PACK, S], BF16, name="h_rows", align_bytes=64)
+        h_planes = keep.tile([P, PACK, S], BF16, name="h_planes", align_bytes=64)
         for t in range(PACK - 1):
-            nc.vector.tensor_copy(h_rows[:, t, :], mem_rows[t][:].indirect(slot_sb[:]))
+            nc.vector.tensor_copy(h_planes[:, t, :], mem_planes[t][:].indirect(slot_sb[:]))
 
         w_bf = keep.tile([P, 2, N, PACK], BF16, name="w_bf", align_bytes=64)
         for i, raw in enumerate((ar_raw, w1_raw)):
-            nc.scalar.copy(w_bf[:, i, :, :], raw[:].rearrange("p t n -> p n t"))
+            nc.scalar.activation(w_bf[:, i, :, :], raw[:].rearrange("p t n -> p n t"), COPY)
         w_code = keep.tile([P, 2 * N], U32, name="w_code", align_bytes=64)
         w_scale = keep.tile([P, 2 * N], U8, name="w_scale", align_bytes=64)
-        nc.vector.quantize_mx(out=w_code[:].bitcast(FP8X4), scales=w_scale[:], in_=w_bf[:].rearrange("p i n t -> p (i n t)"))
+        nc.vector.quantize_mx(
+            out=w_code[:].bitcast(FP8X4), scales=w_scale[:], in_=w_bf[:].rearrange("p i n t -> p (i n t)")
+        )
 
-        for a, b in ((0, 128), (128, 256), (256, 512)):
-            nc.vector.tensor_copy(h_rows[:, PACK - 1, a:b], mem_rows[PACK - 1][:].indirect(slot_sb[:, a // 16 : b // 16]))
-        pieces = ((0, 128), (128, 256), (256, 384), (384, 512))
+        for a, b in LAST_PLANE_CUTS:
+            nc.vector.tensor_copy(h_planes[:, PACK - 1, a:b], mem_planes[PACK - 1][:].indirect(entries(slot_sb, a, b)))
+
         h_bf = []
-        for a, b in pieces:
-            grouped = keep.tile([P, b - a, PACK], BF16, name="h_bf%d" % a, align_bytes=64)
-            for c in range(a, b, 128):
-                nc.scalar.copy(grouped[:, c - a : c - a + 128, :], h_rows[:, :, c : c + 128].rearrange("p t c -> p c t"))
+        for c in range(PIECES):
+            grouped = keep.tile([P, PIECE, PACK], BF16, name="h_bf%d" % c, align_bytes=64)
+            nc.scalar.copy(grouped[:], h_planes[:, :, c * PIECE : (c + 1) * PIECE].rearrange("p t j -> p j t"))
             h_bf.append(grouped)
 
-        h_code, h_scale = [], []
         x_code = keep.tile([P, S], U32, name="x_code", align_bytes=64)
-        for n, (a, b) in enumerate(pieces):
-            code = keep.tile([P, b - a], U32, name="h_code%d" % a, align_bytes=64)
-            scale = keep.tile([P, b - a], U8, name="h_scale%d" % a, align_bytes=64)
-            nc.vector.quantize_mx(out=code[:].bitcast(FP8X4), scales=scale[:], in_=h_bf[n][:].rearrange("p c t -> p (c t)"))
+        h_code, h_scale = [], []
+        for c in range(PIECES):
+            code = keep.tile([P, PIECE], U32, name="h_code%d" % c, align_bytes=64)
+            scale = keep.tile([P, PIECE], U8, name="h_scale%d" % c, align_bytes=64)
+            nc.vector.quantize_mx(
+                out=code[:].bitcast(FP8X4), scales=scale[:], in_=h_bf[c][:].rearrange("p j t -> p (j t)")
+            )
             h_code.append(code)
             h_scale.append(scale)
-            if n == 0:
-                for xa, xb in ((0, 256), (256, 512)):
-                    nc.vector.tensor_copy(x_code[:, xa:xb], word_table[:].bitcast(U32).indirect(offs_sb[:, xa // 16 : xb // 16]))
-        for n, (a, b) in enumerate(pieces):
-            acc = psum.tile([P, b - a], F32, name="acc%d" % a)
-            nc.tensor.matmul_mx(out=acc[:], lhsT=w_code[:, N : 2 * N].bitcast(FP8X4), lhsT_scale=w_scale[:, N : 2 * N],
-                                rhs=x_code[:, a:b].bitcast(FP8X4), rhs_scale=x_scale[:, a:b], start=True, stop=False)
-            nc.tensor.matmul_mx(out=acc[:], lhsT=w_code[:, 0:N].bitcast(FP8X4), lhsT_scale=w_scale[:, 0:N],
-                                rhs=h_code[n][:].bitcast(FP8X4), rhs_scale=h_scale[n][:], start=False, stop=True)
-            result = keep.tile([P, b - a], F32, name="result%d" % a)
+            if c < len(WORD_CUTS):
+                a, b = WORD_CUTS[c]
+                nc.vector.tensor_copy(x_code[:, a:b], word_table[:].bitcast(U32).indirect(entries(offs_sb, a, b)))
+
+        for c in range(PIECES):
+            cols = slice(c * PIECE, (c + 1) * PIECE)
+            input_pass = (w_code[:, N : 2 * N], w_scale[:, N : 2 * N], x_code[:, cols], x_scale[:, cols])
+            memory_pass = (w_code[:, 0:N], w_scale[:, 0:N], h_code[c][:], h_scale[c][:])
+            passes = (memory_pass, input_pass) if c == 0 else (input_pass, memory_pass)
+            acc = psum.tile([N, PIECE], F32, name="acc%d" % c)
+            for i, (weight, weight_scale, moving, moving_scale) in enumerate(passes):
+                nc.tensor.matmul_mx(
+                    out=acc[:],
+                    lhsT=weight.bitcast(FP8X4),
+                    lhsT_scale=weight_scale,
+                    rhs=moving.bitcast(FP8X4),
+                    rhs_scale=moving_scale,
+                    start=(i == 0),
+                    stop=(i == len(passes) - 1),
+                )
+            result = keep.tile([N, PIECE], F32, name="result%d" % c)
             nc.scalar.activation(result[:], acc[:], TANH, bias=bias_sb[:])
-            nc.sync.dma_start(out[:, a:b], result[:])
+            nc.sync.dma_start(out[:, cols], result[:])

@@ -44,78 +44,124 @@ def tile_picked_ylmu_rnn_p_kernel(tc, x_words, x_scales, mem, w1, ar, bias, offs
             return list_tile[:, a // LIST_ROWS : b // LIST_ROWS]
 
         nc.vector.memset(scale_table[:].bitcast(I32), 0)
-
         mem_view = mem.rearrange("(p t) u -> p t u", t=PACK)
         nc.sync.dma_start(offs_sb[:], offs)
         nc.sync.dma_start(slot_sb[:], slot)
+        nc.sync.dma_start(scale_table[0:16, :].bitcast(I32), x_scales[0].bitcast(I32))
+        nc.sync.dma_start(mem_planes[0][:], mem_view[:, 0, :])
+        nc.sync.dma_start(mem_planes[1][:], mem_view[:, 1, :])
+        nc.sync.dma_start(mem_planes[2][:], mem_view[:, 2, :])
         nc.sync.dma_start(ar_raw[:], ar.rearrange("(p t) n -> p t n", t=PACK))
-        for q in range(QUADRANTS):
-            nc.sync.dma_start(
-                scale_table[32 * q : 32 * q + 4, :].bitcast(I32),
-                x_scales[0, 4 * q : 4 * q + 4, :].bitcast(I32),
-            )
-        for t in range(PACK - 1):
-            nc.sync.dma_start(mem_planes[t][:], mem_view[:, t, :])
-        nc.sync.dma_start(w1_raw[:], w1.rearrange("(p t) n -> p t n", t=PACK))
-        nc.sync.dma_start(mem_planes[PACK - 1][:], mem_view[:, PACK - 1, :])
-        nc.sync.dma_start(word_table[:], x_words[0].rearrange("p c t -> p (c t)").bitcast(I32))
-        nc.sync.dma_start(bias_sb[:], bias)
+        nc.sync.dma_start(mem_planes[3][:], mem_view[:, 3, :])
 
         x_scale = keep.tile([P, S], U8, name="x_scale", align_bytes=64)
-        nc.vector.tensor_copy(x_scale[:], scale_table[:].indirect(offs_sb[:]))
-
+        picked_scale = keep.tile([P, S], U8, name="picked_scale", align_bytes=64)
+        nc.vector.memset(x_scale[:].bitcast(I32), 0)
+        x_code = {}
         h_planes = keep.tile([P, PACK, S], BF16, name="h_planes", align_bytes=64)
-        for t in range(PACK - 1):
-            nc.vector.tensor_copy(h_planes[:, t, :], mem_planes[t][:].indirect(slot_sb[:]))
+        h_bf = [keep.tile([P, PIECE, PACK], BF16, name="h_bf%d" % c, align_bytes=64)[:] for c in range(1)]
+        h_code = {}
+        h_scale = [keep.tile([P, PIECE], U8, name="h_scale%d" % c, align_bytes=64) for c in range(PIECES)]
+        w_bf = [keep.tile([P, N, PACK], BF16, name="w_bf%d" % i, align_bytes=64) for i in range(2)]
+        w_code = [keep.tile([P, N], U32, name="w_code%d" % i, align_bytes=64) for i in range(2)]
+        w_scale = [keep.tile([P, N], U8, name="w_scale%d" % i, align_bytes=64) for i in range(2)]
+        acc = [psum.tile([N, PIECE], F32, name="acc%d" % c) for c in range(PIECES)]
+        result = [keep.tile([N, PIECE], F32, name="result%d" % c) for c in range(PIECES)]
+        w_raw = (ar_raw, w1_raw)
 
-        w_bf = keep.tile([P, 2, N, PACK], BF16, name="w_bf", align_bytes=64)
-        for i, raw in enumerate((ar_raw, w1_raw)):
-            nc.scalar.activation(w_bf[:, i, :, :], raw[:].rearrange("p t n -> p n t"), COPY)
-        w_code = keep.tile([P, 2 * N], U32, name="w_code", align_bytes=64)
-        w_scale = keep.tile([P, 2 * N], U8, name="w_scale", align_bytes=64)
-        nc.vector.quantize_mx(
-            out=w_code[:].bitcast(FP8X4), scales=w_scale[:], in_=w_bf[:].rearrange("p i n t -> p (i n t)")
-        )
+        def gather_scales():
+            nc.vector.tensor_copy(picked_scale[:], scale_table[:].indirect(offs_sb[:]))
+            for q in range(QUADRANTS):
+                nc.sync.dma_start(x_scale[32 * q : 32 * q + 4, :].bitcast(I32), picked_scale[4 * q : 4 * q + 4, :].bitcast(I32))
+            nc.sync.dma_start(w1_raw[:], w1.rearrange("(p t) n -> p t n", t=PACK))
+            nc.sync.dma_start(word_table[:], x_words[0].rearrange("p c t -> p (c t)").bitcast(I32))
+            nc.sync.dma_start(bias_sb[:], bias)
 
-        for a, b in LAST_PLANE_CUTS:
-            nc.vector.tensor_copy(h_planes[:, PACK - 1, a:b], mem_planes[PACK - 1][:].indirect(entries(slot_sb, a, b)))
+        def gather_plane(t, a, b):
+            nc.vector.tensor_copy(h_planes[:, t, a:b], mem_planes[t][:].indirect(entries(slot_sb, a, b)))
 
-        h_bf = []
-        for c in range(PIECES):
-            grouped = keep.tile([P, PIECE, PACK], BF16, name="h_bf%d" % c, align_bytes=64)
-            nc.scalar.copy(grouped[:], h_planes[:, :, c * PIECE : (c + 1) * PIECE].rearrange("p t j -> p j t"))
-            h_bf.append(grouped)
+        def gather_words(a, b):
+            words = keep.tile([P, b - a], U32, name="codes%d" % a, align_bytes=64)
+            nc.vector.tensor_copy(words[:], word_table[:].bitcast(U32).indirect(entries(offs_sb, a, b)))
+            for c in range(a // PIECE, b // PIECE):
+                x_code[c] = words[:, c * PIECE - a : (c + 1) * PIECE - a]
 
-        x_code = keep.tile([P, S], U32, name="x_code", align_bytes=64)
-        h_code, h_scale = [], []
-        for c in range(PIECES):
-            code = keep.tile([P, PIECE], U32, name="h_code%d" % c, align_bytes=64)
-            scale = keep.tile([P, PIECE], U8, name="h_scale%d" % c, align_bytes=64)
-            nc.vector.quantize_mx(
-                out=code[:].bitcast(FP8X4), scales=scale[:], in_=h_bf[c][:].rearrange("p j t -> p (j t)")
+        def lay(c, t0, t1):
+            nc.scalar.copy(
+                h_bf[c].rearrange("p (g i) t -> p g t i", i=4),
+                h_planes[:, :, c * PIECE : (c + 1) * PIECE].rearrange("p t (g i) -> p g t i", i=4),
             )
-            h_code.append(code)
-            h_scale.append(scale)
-            if c < len(WORD_CUTS):
-                a, b = WORD_CUTS[c]
-                nc.vector.tensor_copy(x_code[:, a:b], word_table[:].bitcast(U32).indirect(entries(offs_sb, a, b)))
 
-        for c in range(PIECES):
+        def round_weight(i):
+            nc.scalar.activation(w_bf[i][:], w_raw[i][:].rearrange("p t n -> p n t"), COPY)
+
+        def take_over_w1_buffer():
+            late = keep.tile([P, (PIECES - 1) * PIECE, PACK], BF16, name="w1_raw", align_bytes=64)
+            for c in range(PIECES - 1):
+                h_bf.append(late[:, c * PIECE : (c + 1) * PIECE, :])
+
+        def round_weight_on_vector(i):
+            nc.vector.tensor_copy(w_bf[i][:], w_raw[i][:].rearrange("p t n -> p n t"))
+
+        def quantise_weight(i):
+            nc.vector.quantize_mx(out=w_code[i][:].bitcast(FP8X4), scales=w_scale[i][:], in_=w_bf[i][:].rearrange("p n t -> p (n t)"))
+
+        def quantise_h(c, codes=None):
+            if codes is None:
+                codes = keep.tile([P, PIECE], U32, name="h_code%d" % c, align_bytes=64)[:]
+            h_code[c] = codes
+            nc.vector.quantize_mx(out=codes.bitcast(FP8X4), scales=h_scale[c][:], in_=h_bf[c].rearrange("p j t -> p (j t)"))
+
+        def multiply(c, i, start):
             cols = slice(c * PIECE, (c + 1) * PIECE)
-            input_pass = (w_code[:, N : 2 * N], w_scale[:, N : 2 * N], x_code[:, cols], x_scale[:, cols])
-            memory_pass = (w_code[:, 0:N], w_scale[:, 0:N], h_code[c][:], h_scale[c][:])
-            passes = (memory_pass, input_pass) if c == 0 else (input_pass, memory_pass)
-            acc = psum.tile([N, PIECE], F32, name="acc%d" % c)
-            for i, (weight, weight_scale, moving, moving_scale) in enumerate(passes):
-                nc.tensor.matmul_mx(
-                    out=acc[:],
-                    lhsT=weight.bitcast(FP8X4),
-                    lhsT_scale=weight_scale,
-                    rhs=moving.bitcast(FP8X4),
-                    rhs_scale=moving_scale,
-                    start=(i == 0),
-                    stop=(i == len(passes) - 1),
-                )
-            result = keep.tile([N, PIECE], F32, name="result%d" % c)
-            nc.scalar.activation(result[:], acc[:], TANH, bias=bias_sb[:])
-            nc.sync.dma_start(out[:, cols], result[:])
+            moving, moving_scale = (h_code[c], h_scale[c][:]) if i == 0 else (x_code[c], x_scale[:, cols])
+            nc.tensor.matmul_mx(
+                out=acc[c][:],
+                lhsT=w_code[i][:].bitcast(FP8X4),
+                lhsT_scale=w_scale[i][:],
+                rhs=moving.bitcast(FP8X4),
+                rhs_scale=moving_scale,
+                start=start,
+                stop=not start,
+            )
+
+        def finish(c):
+            nc.scalar.activation(result[c][:], acc[c][:], TANH, bias=bias_sb[:])
+            nc.sync.dma_start(out[:, c * PIECE : (c + 1) * PIECE], result[c][:])
+
+        gather_scales()
+        gather_plane(0, 0, 512)
+        gather_plane(1, 0, 512)
+        round_weight(0)
+        gather_plane(2, 0, 512)
+        quantise_weight(0)
+        gather_plane(3, 0, 128)
+        gather_plane(3, 128, 256)
+        gather_plane(3, 256, 512)
+        lay(0, 0, 4)
+        round_weight(1)
+        take_over_w1_buffer()
+        lay(1, 0, 4)
+        lay(2, 0, 4)
+        lay(3, 0, 4)
+        quantise_h(0)
+        quantise_weight(1)
+        multiply(0, 0, True)
+        gather_words(0, 128)
+        gather_words(128, 384)
+        gather_words(384, 512)
+        multiply(0, 1, False)
+        finish(0)
+        multiply(1, 1, True)
+        multiply(2, 1, True)
+        multiply(3, 1, True)
+        late_codes = keep.tile([P, 3 * PIECE], U32, name="codes0", align_bytes=64)
+        quantise_h(1, late_codes[:, 0:PIECE])
+        multiply(1, 0, False)
+        finish(1)
+        quantise_h(2, late_codes[:, PIECE : 2 * PIECE])
+        multiply(2, 0, False)
+        finish(2)
+        quantise_h(3, late_codes[:, 2 * PIECE : 3 * PIECE])
+        multiply(3, 0, False)
+        finish(3)

@@ -51,15 +51,17 @@ def tile_picked_ylmu_rnn_p_kernel(tc, x_words, x_scales, mem, w1, ar, bias, offs
         nc.sync.dma_start(mem_planes[0][:], mem_view[:, 0, :])
         nc.sync.dma_start(mem_planes[1][:], mem_view[:, 1, :])
         nc.sync.dma_start(mem_planes[2][:], mem_view[:, 2, :])
-        nc.sync.dma_start(ar_raw[:], ar.rearrange("(p t) n -> p t n", t=PACK))
         nc.sync.dma_start(mem_planes[3][:], mem_view[:, 3, :])
+        nc.sync.dma_start(ar_raw[:], ar.rearrange("(p t) n -> p t n", t=PACK))
 
         x_scale = keep.tile([P, S], U8, name="x_scale", align_bytes=64)
         picked_scale = keep.tile([P, S], U8, name="picked_scale", align_bytes=64)
         nc.vector.memset(x_scale[:].bitcast(I32), 0)
         x_code = {}
-        h_planes = keep.tile([P, PACK, S], BF16, name="h_planes", align_bytes=64)
-        h_bf = [keep.tile([P, PIECE, PACK], BF16, name="h_bf%d" % c, align_bytes=64)[:] for c in range(1)]
+        h_pairs = keep.tile([P, 2 * S * 2], BF16, name="h_pairs", align_bytes=64)
+        pair_values = h_pairs[:].rearrange("p (u j e) -> p u j e", u=2, e=2)
+        pair_words = h_pairs[:].bitcast(U32).rearrange("p (u j) -> p u j", u=2)
+        h_bf = [keep.tile([P, PIECE, PACK], BF16, name="h_bf%d" % c, align_bytes=64) for c in range(PIECES)]
         h_code = {}
         h_scale = [keep.tile([P, PIECE], U8, name="h_scale%d" % c, align_bytes=64) for c in range(PIECES)]
         w_bf = [keep.tile([P, N, PACK], BF16, name="w_bf%d" % i, align_bytes=64) for i in range(2)]
@@ -78,7 +80,7 @@ def tile_picked_ylmu_rnn_p_kernel(tc, x_words, x_scales, mem, w1, ar, bias, offs
             nc.sync.dma_start(bias_sb[:], bias)
 
         def gather_plane(t, a, b):
-            nc.vector.tensor_copy(h_planes[:, t, a:b], mem_planes[t][:].indirect(entries(slot_sb, a, b)))
+            nc.vector.tensor_copy(pair_values[:, t // 2, a:b, t % 2], mem_planes[t][:].indirect(entries(slot_sb, a, b)))
 
         def gather_words(a, b):
             words = keep.tile([P, b - a], U32, name="codes%d" % a, align_bytes=64)
@@ -88,20 +90,15 @@ def tile_picked_ylmu_rnn_p_kernel(tc, x_words, x_scales, mem, w1, ar, bias, offs
 
         def lay(c, t0, t1):
             nc.scalar.copy(
-                h_bf[c].rearrange("p (g i) t -> p g t i", i=4),
-                h_planes[:, :, c * PIECE : (c + 1) * PIECE].rearrange("p t (g i) -> p g t i", i=4),
+                h_bf[c][:].rearrange("p j t -> p (j t)").bitcast(U32).rearrange("p (g i u) -> p g u i", i=4, u=2),
+                pair_words[:, :, c * PIECE : (c + 1) * PIECE].rearrange("p u (g i) -> p g u i", i=4),
             )
 
         def round_weight(i):
-            nc.scalar.activation(w_bf[i][:], w_raw[i][:].rearrange("p t n -> p n t"), COPY)
-
-        def take_over_w1_buffer():
-            late = keep.tile([P, (PIECES - 1) * PIECE, PACK], BF16, name="w1_raw", align_bytes=64)
-            for c in range(PIECES - 1):
-                h_bf.append(late[:, c * PIECE : (c + 1) * PIECE, :])
+            nc.scalar.activation(w_bf[i][:].rearrange("p (g i) t -> p g t i", i=4), w_raw[i][:].rearrange("p t (g i) -> p g t i", i=4), COPY)
 
         def round_weight_on_vector(i):
-            nc.vector.tensor_copy(w_bf[i][:], w_raw[i][:].rearrange("p t n -> p n t"))
+            nc.vector.tensor_copy(w_bf[i][:].rearrange("p (g i) t -> p g t i", i=4), w_raw[i][:].rearrange("p t (g i) -> p g t i", i=4))
 
         def quantise_weight(i):
             nc.vector.quantize_mx(out=w_code[i][:].bitcast(FP8X4), scales=w_scale[i][:], in_=w_bf[i][:].rearrange("p n t -> p (n t)"))
@@ -110,7 +107,7 @@ def tile_picked_ylmu_rnn_p_kernel(tc, x_words, x_scales, mem, w1, ar, bias, offs
             if codes is None:
                 codes = keep.tile([P, PIECE], U32, name="h_code%d" % c, align_bytes=64)[:]
             h_code[c] = codes
-            nc.vector.quantize_mx(out=codes.bitcast(FP8X4), scales=h_scale[c][:], in_=h_bf[c].rearrange("p j t -> p (j t)"))
+            nc.vector.quantize_mx(out=codes.bitcast(FP8X4), scales=h_scale[c][:], in_=h_bf[c][:].rearrange("p j t -> p (j t)"))
 
         def multiply(c, i, start):
             cols = slice(c * PIECE, (c + 1) * PIECE)
@@ -132,36 +129,33 @@ def tile_picked_ylmu_rnn_p_kernel(tc, x_words, x_scales, mem, w1, ar, bias, offs
         gather_scales()
         gather_plane(0, 0, 512)
         gather_plane(1, 0, 512)
-        round_weight(0)
         gather_plane(2, 0, 512)
-        quantise_weight(0)
         gather_plane(3, 0, 128)
-        gather_plane(3, 128, 256)
-        gather_plane(3, 256, 512)
+        gather_plane(3, 128, 512)
         lay(0, 0, 4)
-        round_weight(1)
-        take_over_w1_buffer()
+        round_weight(0)
         lay(1, 0, 4)
         lay(2, 0, 4)
         lay(3, 0, 4)
         quantise_h(0)
+        round_weight_on_vector(1)
+        quantise_weight(0)
         quantise_weight(1)
+        quantise_h(1)
+        quantise_h(2)
+        quantise_h(3)
         multiply(0, 0, True)
-        gather_words(0, 128)
-        gather_words(128, 384)
+        multiply(1, 0, True)
+        multiply(2, 0, True)
+        multiply(3, 0, True)
+        gather_words(0, 256)
+        gather_words(256, 384)
         gather_words(384, 512)
         multiply(0, 1, False)
         finish(0)
-        multiply(1, 1, True)
-        multiply(2, 1, True)
-        multiply(3, 1, True)
-        late_codes = keep.tile([P, 3 * PIECE], U32, name="codes0", align_bytes=64)
-        quantise_h(1, late_codes[:, 0:PIECE])
-        multiply(1, 0, False)
+        multiply(1, 1, False)
         finish(1)
-        quantise_h(2, late_codes[:, PIECE : 2 * PIECE])
-        multiply(2, 0, False)
+        multiply(2, 1, False)
         finish(2)
-        quantise_h(3, late_codes[:, 2 * PIECE : 3 * PIECE])
-        multiply(3, 0, False)
+        multiply(3, 1, False)
         finish(3)

@@ -17,12 +17,17 @@ TANH = mybir.ActivationFunctionType.Tanh
 
 P = 128
 PACK = 4
+PAIRS = 2
 QUADRANTS = 4
+QUADRANT = P // QUADRANTS
+SCALE_ROWS = K // 32
+ROWS_A_QUADRANT = SCALE_ROWS // QUADRANTS
 LIST_ROWS = 16
+RUN = 4
 PIECE = 128
 PIECES = S // PIECE
-LAST_PLANE_CUTS = ((0, PIECE), (PIECE, 2 * PIECE), (2 * PIECE, S))
-WORD_CUTS = ((0, 2 * PIECE), (2 * PIECE, 3 * PIECE), (3 * PIECE, S))
+HALF = PIECES // 2
+MEMORY, INPUT = 0, 1
 
 
 def tile_picked_ylmu_rnn_p_kernel(tc, x_words, x_scales, mem, w1, ar, bias, offs, slot, out):
@@ -43,119 +48,117 @@ def tile_picked_ylmu_rnn_p_kernel(tc, x_words, x_scales, mem, w1, ar, bias, offs
         def entries(list_tile, a, b):
             return list_tile[:, a // LIST_ROWS : b // LIST_ROWS]
 
+        def piece(c):
+            return slice(c * PIECE, (c + 1) * PIECE)
+
         nc.vector.memset(scale_table[:].bitcast(I32), 0)
+
         mem_view = mem.rearrange("(p t) u -> p t u", t=PACK)
         nc.sync.dma_start(offs_sb[:], offs)
         nc.sync.dma_start(slot_sb[:], slot)
-        nc.sync.dma_start(scale_table[0:16, :].bitcast(I32), x_scales[0].bitcast(I32))
-        nc.sync.dma_start(mem_planes[0][:], mem_view[:, 0, :])
-        nc.sync.dma_start(mem_planes[1][:], mem_view[:, 1, :])
-        nc.sync.dma_start(mem_planes[2][:], mem_view[:, 2, :])
-        nc.sync.dma_start(mem_planes[3][:], mem_view[:, 3, :])
+        nc.sync.dma_start(scale_table[0:SCALE_ROWS, :].bitcast(I32), x_scales[0].bitcast(I32))
+        for t in range(PACK):
+            nc.sync.dma_start(mem_planes[t][:], mem_view[:, t, :])
         nc.sync.dma_start(ar_raw[:], ar.rearrange("(p t) n -> p t n", t=PACK))
+        nc.sync.dma_start(word_table[:], x_words[0].rearrange("p c t -> p (c t)").bitcast(I32))
 
         x_scale = keep.tile([P, S], U8, name="x_scale", align_bytes=64)
         picked_scale = keep.tile([P, S], U8, name="picked_scale", align_bytes=64)
         nc.vector.memset(x_scale[:].bitcast(I32), 0)
-        x_code = {}
-        h_pairs = keep.tile([P, 2 * S * 2], BF16, name="h_pairs", align_bytes=64)
-        pair_values = h_pairs[:].rearrange("p (u j e) -> p u j e", u=2, e=2)
-        pair_words = h_pairs[:].bitcast(U32).rearrange("p (u j) -> p u j", u=2)
+
+        h_pairs = keep.tile([P, PAIRS * S * PAIRS], BF16, name="h_pairs", align_bytes=64)
+        pair_values = h_pairs[:].rearrange("p (u j e) -> p u j e", u=PAIRS, e=PAIRS)
+        pair_words = h_pairs[:].bitcast(U32).rearrange("p (u j) -> p u j", u=PAIRS)
         h_bf = [keep.tile([P, PIECE, PACK], BF16, name="h_bf%d" % c, align_bytes=64) for c in range(PIECES)]
-        h_code = {}
         h_scale = [keep.tile([P, PIECE], U8, name="h_scale%d" % c, align_bytes=64) for c in range(PIECES)]
-        w_bf = [keep.tile([P, N, PACK], BF16, name="w_bf%d" % i, align_bytes=64) for i in range(2)]
-        w_code = [keep.tile([P, N], U32, name="w_code%d" % i, align_bytes=64) for i in range(2)]
-        w_scale = [keep.tile([P, N], U8, name="w_scale%d" % i, align_bytes=64) for i in range(2)]
+        w_raw = (ar_raw, w1_raw)
+        w_bf = [keep.tile([P, N, PACK], BF16, name="w_bf%d" % i, align_bytes=64) for i in (MEMORY, INPUT)]
+        w_code = [keep.tile([P, N], U32, name="w_code%d" % i, align_bytes=64) for i in (MEMORY, INPUT)]
+        w_scale = [keep.tile([P, N], U8, name="w_scale%d" % i, align_bytes=64) for i in (MEMORY, INPUT)]
         acc = [psum.tile([N, PIECE], F32, name="acc%d" % c) for c in range(PIECES)]
         result = [keep.tile([N, PIECE], F32, name="result%d" % c) for c in range(PIECES)]
-        w_raw = (ar_raw, w1_raw)
-
-        def gather_scales():
-            nc.vector.tensor_copy(picked_scale[:], scale_table[:].indirect(offs_sb[:]))
-            for q in range(QUADRANTS):
-                nc.sync.dma_start(x_scale[32 * q : 32 * q + 4, :].bitcast(I32), picked_scale[4 * q : 4 * q + 4, :].bitcast(I32))
-            nc.sync.dma_start(w1_raw[:], w1.rearrange("(p t) n -> p t n", t=PACK))
-            nc.sync.dma_start(word_table[:], x_words[0].rearrange("p c t -> p (c t)").bitcast(I32))
-            nc.sync.dma_start(bias_sb[:], bias)
 
         def gather_plane(t, a, b):
-            nc.vector.tensor_copy(pair_values[:, t // 2, a:b, t % 2], mem_planes[t][:].indirect(entries(slot_sb, a, b)))
+            nc.vector.tensor_copy(
+                pair_values[:, t // PAIRS, a:b, t % PAIRS], mem_planes[t][:].indirect(entries(slot_sb, a, b))
+            )
 
-        def gather_words(a, b):
-            words = keep.tile([P, b - a], U32, name="codes%d" % a, align_bytes=64)
-            nc.vector.tensor_copy(words[:], word_table[:].bitcast(U32).indirect(entries(offs_sb, a, b)))
-            for c in range(a // PIECE, b // PIECE):
-                x_code[c] = words[:, c * PIECE - a : (c + 1) * PIECE - a]
+        def gather_words(words, a, b):
+            nc.vector.tensor_copy(words, word_table[:].bitcast(U32).indirect(entries(offs_sb, a, b)))
 
-        def lay(c, t0, t1):
+        def join_pairs(c):
+            joined = h_bf[c][:].rearrange("p j t -> p (j t)").bitcast(U32)
             nc.scalar.copy(
-                h_bf[c][:].rearrange("p j t -> p (j t)").bitcast(U32).rearrange("p (g i u) -> p g u i", i=4, u=2),
-                pair_words[:, :, c * PIECE : (c + 1) * PIECE].rearrange("p u (g i) -> p g u i", i=4),
+                joined.rearrange("p (g i u) -> p g u i", i=RUN, u=PAIRS),
+                pair_words[:, :, piece(c)].rearrange("p u (g i) -> p g u i", i=RUN),
             )
 
         def round_weight(i):
-            nc.scalar.activation(w_bf[i][:].rearrange("p (g i) t -> p g t i", i=4), w_raw[i][:].rearrange("p t (g i) -> p g t i", i=4), COPY)
+            nc.scalar.activation(
+                w_bf[i][:].rearrange("p (g i) t -> p g t i", i=RUN),
+                w_raw[i][:].rearrange("p t (g i) -> p g t i", i=RUN),
+                COPY,
+            )
 
-        def round_weight_on_vector(i):
-            nc.vector.tensor_copy(w_bf[i][:].rearrange("p (g i) t -> p g t i", i=4), w_raw[i][:].rearrange("p t (g i) -> p g t i", i=4))
+        def quantise(code, scale, values):
+            nc.vector.quantize_mx(out=code.bitcast(FP8X4), scales=scale, in_=values.rearrange("p c t -> p (c t)"))
 
-        def quantise_weight(i):
-            nc.vector.quantize_mx(out=w_code[i][:].bitcast(FP8X4), scales=w_scale[i][:], in_=w_bf[i][:].rearrange("p n t -> p (n t)"))
-
-        def quantise_h(c, codes=None):
-            if codes is None:
-                codes = keep.tile([P, PIECE], U32, name="h_code%d" % c, align_bytes=64)[:]
-            h_code[c] = codes
-            nc.vector.quantize_mx(out=codes.bitcast(FP8X4), scales=h_scale[c][:], in_=h_bf[c][:].rearrange("p j t -> p (j t)"))
-
-        def multiply(c, i, start):
-            cols = slice(c * PIECE, (c + 1) * PIECE)
-            moving, moving_scale = (h_code[c], h_scale[c][:]) if i == 0 else (x_code[c], x_scale[:, cols])
+        def multiply(c, i, moving, moving_scale):
             nc.tensor.matmul_mx(
                 out=acc[c][:],
                 lhsT=w_code[i][:].bitcast(FP8X4),
                 lhsT_scale=w_scale[i][:],
                 rhs=moving.bitcast(FP8X4),
                 rhs_scale=moving_scale,
-                start=start,
-                stop=not start,
+                start=(i == MEMORY),
+                stop=(i == INPUT),
             )
 
-        def finish(c):
-            nc.scalar.activation(result[c][:], acc[c][:], TANH, bias=bias_sb[:])
-            nc.sync.dma_start(out[:, c * PIECE : (c + 1) * PIECE], result[c][:])
+        nc.vector.tensor_copy(picked_scale[:], scale_table[:].indirect(offs_sb[:]))
+        for q in range(QUADRANTS):
+            nc.sync.dma_start(
+                x_scale[QUADRANT * q : QUADRANT * q + ROWS_A_QUADRANT, :].bitcast(I32),
+                picked_scale[ROWS_A_QUADRANT * q : ROWS_A_QUADRANT * (q + 1), :].bitcast(I32),
+            )
+        nc.sync.dma_start(w1_raw[:], w1.rearrange("(p t) n -> p t n", t=PACK))
+        nc.sync.dma_start(bias_sb[:], bias)
 
-        gather_scales()
-        gather_plane(0, 0, 512)
-        gather_plane(1, 0, 512)
-        gather_plane(2, 0, 512)
-        gather_plane(3, 0, 128)
-        gather_plane(3, 128, 512)
-        lay(0, 0, 4)
-        round_weight(0)
-        lay(1, 0, 4)
-        lay(2, 0, 4)
-        lay(3, 0, 4)
-        quantise_h(0)
-        round_weight_on_vector(1)
-        quantise_weight(0)
-        quantise_weight(1)
-        quantise_h(1)
-        quantise_h(2)
-        quantise_h(3)
-        multiply(0, 0, True)
-        multiply(1, 0, True)
-        multiply(2, 0, True)
-        multiply(3, 0, True)
-        gather_words(0, 256)
-        gather_words(256, 384)
-        gather_words(384, 512)
-        multiply(0, 1, False)
-        finish(0)
-        multiply(1, 1, False)
-        finish(1)
-        multiply(2, 1, False)
-        finish(2)
-        multiply(3, 1, False)
-        finish(3)
+        for t in range(PACK - 1):
+            gather_plane(t, 0, S)
+        gather_plane(PACK - 1, 0, PIECE)
+        gather_plane(PACK - 1, PIECE, S)
+
+        join_pairs(0)
+        round_weight(MEMORY)
+        for c in range(1, PIECES):
+            join_pairs(c)
+        round_weight(INPUT)
+
+        early_codes = []
+        for c in range(HALF):
+            code = keep.tile([P, PIECE], U32, name="h_code%d" % c, align_bytes=64)
+            quantise(code[:], h_scale[c][:], h_bf[c][:])
+            early_codes.append(code)
+            if c == 0:
+                quantise(w_code[MEMORY][:], w_scale[MEMORY][:], w_bf[MEMORY][:])
+        for c in range(HALF):
+            multiply(c, MEMORY, early_codes[c][:], h_scale[c][:])
+
+        early_words = keep.tile([P, HALF * PIECE], U32, name="ar_raw", align_bytes=64)
+        gather_words(early_words[:], 0, HALF * PIECE)
+
+        late_codes = keep.tile([P, HALF * PIECE], U32, name="picked_scale", align_bytes=64)
+        for c in range(HALF):
+            quantise(late_codes[:, piece(c)], h_scale[HALF + c][:], h_bf[HALF + c][:])
+            multiply(HALF + c, MEMORY, late_codes[:, piece(c)], h_scale[HALF + c][:])
+
+        quantise(w_code[INPUT][:], w_scale[INPUT][:], w_bf[INPUT][:])
+        late_words = keep.tile([P, HALF * PIECE], U32, name="w1_raw", align_bytes=64)
+        for c in range(HALF):
+            gather_words(late_words[:, piece(c)], (HALF + c) * PIECE, (HALF + c + 1) * PIECE)
+
+        for c in range(PIECES):
+            words = (early_words, late_words)[c // HALF]
+            multiply(c, INPUT, words[:, piece(c % HALF)], x_scale[:, piece(c)])
+            nc.scalar.activation(result[c][:], acc[c][:], TANH, bias=bias_sb[:])
+            nc.sync.dma_start(out[:, piece(c)], result[c][:])

@@ -27,6 +27,7 @@ RUN = 4
 PIECE = 128
 PIECES = S // PIECE
 HALF = PIECES // 2
+JOIN_CUTS = ((0, PIECE), (PIECE, HALF * PIECE), (HALF * PIECE, S))
 MEMORY, INPUT = 0, 1
 
 
@@ -69,8 +70,11 @@ def tile_picked_ylmu_rnn_p_kernel(tc, x_words, x_scales, mem, w1, ar, bias, offs
         h_pairs = keep.tile([P, PAIRS * S * PAIRS], BF16, name="h_pairs", align_bytes=64)
         pair_values = h_pairs[:].rearrange("p (u j e) -> p u j e", u=PAIRS, e=PAIRS)
         pair_words = h_pairs[:].bitcast(U32).rearrange("p (u j) -> p u j", u=PAIRS)
-        h_bf = [keep.tile([P, PIECE, PACK], BF16, name="h_bf%d" % c, align_bytes=64) for c in range(PIECES)]
-        h_scale = [keep.tile([P, PIECE], U8, name="h_scale%d" % c, align_bytes=64) for c in range(PIECES)]
+        first_planes = keep.tile([P, PAIRS, S], BF16, name="first_planes", align_bytes=64)
+        h_bf = [keep.tile([P, PIECE, PACK], BF16, name="h_bf%d" % c, align_bytes=64) for c in range(HALF)]
+        h_scale = [keep.tile([P, PIECE], U8, name="h_scale%d" % c, align_bytes=64) for c in range(HALF)]
+        late_bf = keep.tile([P, HALF * PIECE, PACK], BF16, name="late_bf", align_bytes=64)
+        late_scale = keep.tile([P, HALF * PIECE], U8, name="late_scale", align_bytes=64)
         w_raw = (ar_raw, w1_raw)
         w_bf = [keep.tile([P, N, PACK], BF16, name="w_bf%d" % i, align_bytes=64) for i in (MEMORY, INPUT)]
         w_code = [keep.tile([P, N], U32, name="w_code%d" % i, align_bytes=64) for i in (MEMORY, INPUT)]
@@ -78,19 +82,17 @@ def tile_picked_ylmu_rnn_p_kernel(tc, x_words, x_scales, mem, w1, ar, bias, offs
         acc = [psum.tile([N, PIECE], F32, name="acc%d" % c) for c in range(PIECES)]
         result = [keep.tile([N, PIECE], F32, name="result%d" % c) for c in range(PIECES)]
 
-        def gather_plane(t, a, b):
-            nc.vector.tensor_copy(
-                pair_values[:, t // PAIRS, a:b, t % PAIRS], mem_planes[t][:].indirect(entries(slot_sb, a, b))
-            )
+        def gather_plane(target, t, a, b):
+            nc.vector.tensor_copy(target[:, a:b], mem_planes[t][:].indirect(entries(slot_sb, a, b)))
 
         def gather_words(words, a, b):
             nc.vector.tensor_copy(words, word_table[:].bitcast(U32).indirect(entries(offs_sb, a, b)))
 
-        def join_pairs(c):
-            joined = h_bf[c][:].rearrange("p j t -> p (j t)").bitcast(U32)
+        def join_pairs(values, a, b):
+            joined = values.rearrange("p j t -> p (j t)").bitcast(U32)
             nc.scalar.copy(
                 joined.rearrange("p (g i u) -> p g u i", i=RUN, u=PAIRS),
-                pair_words[:, :, piece(c)].rearrange("p u (g i) -> p g u i", i=RUN),
+                pair_words[:, :, a:b].rearrange("p u (g i) -> p g u i", i=RUN),
             )
 
         def round_weight(i):
@@ -123,15 +125,20 @@ def tile_picked_ylmu_rnn_p_kernel(tc, x_words, x_scales, mem, w1, ar, bias, offs
         nc.sync.dma_start(w1_raw[:], w1.rearrange("(p t) n -> p t n", t=PACK))
         nc.sync.dma_start(bias_sb[:], bias)
 
-        for t in range(PACK - 1):
-            gather_plane(t, 0, S)
-        gather_plane(PACK - 1, 0, PIECE)
-        gather_plane(PACK - 1, PIECE, S)
+        for e in range(PAIRS):
+            gather_plane(first_planes[:, e, :], e, 0, S)
+        nc.scalar.copy(
+            pair_values[:, 0, :, :].rearrange("p (g i) e -> p g e i", i=RUN),
+            first_planes[:].rearrange("p e (g i) -> p g e i", i=RUN),
+        )
+        gather_plane(pair_values[:, 1, :, 0], PACK - 2, 0, S)
+        for a, b in JOIN_CUTS:
+            gather_plane(pair_values[:, 1, :, 1], PACK - 1, a, b)
 
-        join_pairs(0)
+        join_pairs(h_bf[0][:], *JOIN_CUTS[0])
         round_weight(MEMORY)
-        for c in range(1, PIECES):
-            join_pairs(c)
+        join_pairs(h_bf[1][:], *JOIN_CUTS[1])
+        join_pairs(late_bf[:], *JOIN_CUTS[2])
         round_weight(INPUT)
 
         early_codes = []
@@ -144,21 +151,20 @@ def tile_picked_ylmu_rnn_p_kernel(tc, x_words, x_scales, mem, w1, ar, bias, offs
         for c in range(HALF):
             multiply(c, MEMORY, early_codes[c][:], h_scale[c][:])
 
-        early_words = keep.tile([P, HALF * PIECE], U32, name="ar_raw", align_bytes=64)
-        gather_words(early_words[:], 0, HALF * PIECE)
+        early_words = keep.tile([P, S - PIECE], U32, name="ar_raw", align_bytes=64)
+        gather_words(early_words[:], 0, S - PIECE)
 
         late_codes = keep.tile([P, HALF * PIECE], U32, name="picked_scale", align_bytes=64)
+        quantise(late_codes[:], late_scale[:], late_bf[:])
         for c in range(HALF):
-            quantise(late_codes[:, piece(c)], h_scale[HALF + c][:], h_bf[HALF + c][:])
-            multiply(HALF + c, MEMORY, late_codes[:, piece(c)], h_scale[HALF + c][:])
+            multiply(HALF + c, MEMORY, late_codes[:, piece(c)], late_scale[:, piece(c)])
 
         quantise(w_code[INPUT][:], w_scale[INPUT][:], w_bf[INPUT][:])
-        late_words = keep.tile([P, HALF * PIECE], U32, name="w1_raw", align_bytes=64)
-        for c in range(HALF):
-            gather_words(late_words[:, piece(c)], (HALF + c) * PIECE, (HALF + c + 1) * PIECE)
+        late_words = keep.tile([P, PIECE], U32, name="w1_raw", align_bytes=64)
+        gather_words(late_words[:], S - PIECE, S)
 
         for c in range(PIECES):
-            words = (early_words, late_words)[c // HALF]
-            multiply(c, INPUT, words[:, piece(c % HALF)], x_scale[:, piece(c)])
+            words = early_words[:, piece(c)] if c < PIECES - 1 else late_words[:]
+            multiply(c, INPUT, words, x_scale[:, piece(c)])
             nc.scalar.activation(result[c][:], acc[c][:], TANH, bias=bias_sb[:])
             nc.sync.dma_start(out[:, piece(c)], result[c][:])

@@ -22,6 +22,7 @@ QUADRANTS = 4
 QUADRANT = P // QUADRANTS
 SCALE_ROWS = K // 32
 ROWS_A_QUADRANT = SCALE_ROWS // QUADRANTS
+FIRST_ROW = P - SCALE_ROWS
 LIST_ROWS = 16
 RUN = 4
 PIECE = 128
@@ -52,14 +53,15 @@ def tile_picked_ylmu_rnn_p_kernel(tc, x_words, x_scales, mem, w1, ar, bias, offs
         def piece(c):
             return slice(c * PIECE, (c + 1) * PIECE)
 
-        nc.vector.memset(scale_table[:].bitcast(I32), 0)
+        nc.vector.memset(scale_table[0:FIRST_ROW, :].bitcast(I32), 0)
 
         mem_view = mem.rearrange("(p t) u -> p t u", t=PACK)
+        nc.sync.dma_start(scale_table[FIRST_ROW:P, :].bitcast(I32), x_scales[0].bitcast(I32))
         nc.sync.dma_start(offs_sb[:], offs)
-        nc.sync.dma_start(slot_sb[:], slot)
-        nc.sync.dma_start(scale_table[0:SCALE_ROWS, :].bitcast(I32), x_scales[0].bitcast(I32))
         for t in range(PACK):
             nc.sync.dma_start(mem_planes[t][:], mem_view[:, t, :])
+            if t == 0:
+                nc.sync.dma_start(slot_sb[:], slot)
         nc.sync.dma_start(ar_raw[:], ar.rearrange("(p t) n -> p t n", t=PACK))
         nc.sync.dma_start(word_table[:], x_words[0].rearrange("p c t -> p (c t)").bitcast(I32))
 
@@ -120,7 +122,7 @@ def tile_picked_ylmu_rnn_p_kernel(tc, x_words, x_scales, mem, w1, ar, bias, offs
         for q in range(QUADRANTS):
             nc.sync.dma_start(
                 x_scale[QUADRANT * q : QUADRANT * q + ROWS_A_QUADRANT, :].bitcast(I32),
-                picked_scale[ROWS_A_QUADRANT * q : ROWS_A_QUADRANT * (q + 1), :].bitcast(I32),
+                picked_scale[FIRST_ROW + ROWS_A_QUADRANT * q : FIRST_ROW + ROWS_A_QUADRANT * (q + 1), :].bitcast(I32),
             )
         nc.sync.dma_start(w1_raw[:], w1.rearrange("(p t) n -> p t n", t=PACK))
         nc.sync.dma_start(bias_sb[:], bias)

@@ -56,7 +56,7 @@ def tile_picked_ylmu_rnn_p_kernel(tc, x_words, x_scales, mem, w1, ar, bias, offs
         nc.vector.memset(scale_table[0:FIRST_ROW, :].bitcast(I32), 0)
 
         mem_view = mem.rearrange("(p t) u -> p t u", t=PACK)
-        nc.sync.dma_start(scale_table[FIRST_ROW:P, :].bitcast(I32), x_scales[0].bitcast(I32))
+        nc.scalar.dma_start(scale_table[FIRST_ROW:P, :].bitcast(I32), x_scales[0].bitcast(I32))
         nc.sync.dma_start(offs_sb[:], offs)
         for t in range(PACK):
             nc.sync.dma_start(mem_planes[t][:], mem_view[:, t, :])

@@ -28,7 +28,7 @@ RUN = 4
 PIECE = 128
 PIECES = S // PIECE
 HALF = PIECES // 2
-JOIN_CUTS = ((0, PIECE), (PIECE, HALF * PIECE), (HALF * PIECE, S))
+JOIN_CUTS = ((0, HALF * PIECE), (HALF * PIECE, S))
 MEMORY, INPUT = 0, 1
 
 
@@ -73,8 +73,9 @@ def tile_picked_ylmu_rnn_p_kernel(tc, x_words, x_scales, mem, w1, ar, bias, offs
         pair_values = h_pairs[:].rearrange("p (u j e) -> p u j e", u=PAIRS, e=PAIRS)
         pair_words = h_pairs[:].bitcast(U32).rearrange("p (u j) -> p u j", u=PAIRS)
         first_planes = keep.tile([P, PAIRS, S], BF16, name="first_planes", align_bytes=64)
-        h_bf = [keep.tile([P, PIECE, PACK], BF16, name="h_bf%d" % c, align_bytes=64) for c in range(HALF)]
-        h_scale = [keep.tile([P, PIECE], U8, name="h_scale%d" % c, align_bytes=64) for c in range(HALF)]
+        early_bf = keep.tile([P, HALF * PIECE, PACK], BF16, name="early_bf", align_bytes=64)
+        early_scale = keep.tile([P, HALF * PIECE], U8, name="early_scale", align_bytes=64)
+        early_codes = keep.tile([P, HALF * PIECE], U32, name="early_codes", align_bytes=64)
         late_bf = keep.tile([P, HALF * PIECE, PACK], BF16, name="late_bf", align_bytes=64)
         late_scale = keep.tile([P, HALF * PIECE], U8, name="late_scale", align_bytes=64)
         w_raw = (ar_raw, w1_raw)
@@ -137,21 +138,15 @@ def tile_picked_ylmu_rnn_p_kernel(tc, x_words, x_scales, mem, w1, ar, bias, offs
         for a, b in JOIN_CUTS:
             gather_plane(pair_values[:, 1, :, 1], PACK - 1, a, b)
 
-        join_pairs(h_bf[0][:], *JOIN_CUTS[0])
         round_weight(MEMORY)
-        join_pairs(h_bf[1][:], *JOIN_CUTS[1])
-        join_pairs(late_bf[:], *JOIN_CUTS[2])
+        join_pairs(early_bf[:], *JOIN_CUTS[0])
+        join_pairs(late_bf[:], *JOIN_CUTS[1])
         round_weight(INPUT)
 
-        early_codes = []
+        quantise(w_code[MEMORY][:], w_scale[MEMORY][:], w_bf[MEMORY][:])
+        quantise(early_codes[:], early_scale[:], early_bf[:])
         for c in range(HALF):
-            code = keep.tile([P, PIECE], U32, name="h_code%d" % c, align_bytes=64)
-            quantise(code[:], h_scale[c][:], h_bf[c][:])
-            early_codes.append(code)
-            if c == 0:
-                quantise(w_code[MEMORY][:], w_scale[MEMORY][:], w_bf[MEMORY][:])
-        for c in range(HALF):
-            multiply(c, MEMORY, early_codes[c][:], h_scale[c][:])
+            multiply(c, MEMORY, early_codes[:, piece(c)], early_scale[:, piece(c)])
 
         early_words = keep.tile([P, S - PIECE], U32, name="ar_raw", align_bytes=64)
         gather_words(early_words[:], 0, S - PIECE)

@@ -120,12 +120,12 @@ def tile_picked_ylmu_rnn_p_kernel(tc, x_words, x_scales, mem, w1, ar, bias, offs
             )
 
         nc.vector.tensor_copy(picked_scale[:], scale_table[:].indirect(offs_sb[:]))
+        nc.sync.dma_start(w1_raw[:], w1.rearrange("(p t) n -> p t n", t=PACK))
         for q in range(QUADRANTS):
             nc.sync.dma_start(
                 x_scale[QUADRANT * q : QUADRANT * q + ROWS_A_QUADRANT, :].bitcast(I32),
                 picked_scale[FIRST_ROW + ROWS_A_QUADRANT * q : FIRST_ROW + ROWS_A_QUADRANT * (q + 1), :].bitcast(I32),
             )
-        nc.sync.dma_start(w1_raw[:], w1.rearrange("(p t) n -> p t n", t=PACK))
         nc.sync.dma_start(bias_sb[:], bias)
 
         for e in range(PAIRS):
@@ -144,14 +144,14 @@ def tile_picked_ylmu_rnn_p_kernel(tc, x_words, x_scales, mem, w1, ar, bias, offs
         round_weight(INPUT)
 
         quantise(w_code[MEMORY][:], w_scale[MEMORY][:], w_bf[MEMORY][:])
+
+        early_words = keep.tile([P, S - PIECE], U32, name="ar_raw", align_bytes=64)
+        gather_words(early_words[:], 0, S - PIECE)
         quantise(early_codes[:], early_scale[:], early_bf[:])
         for c in range(HALF):
             multiply(c, MEMORY, early_codes[:, piece(c)], early_scale[:, piece(c)])
 
-        early_words = keep.tile([P, S - PIECE], U32, name="ar_raw", align_bytes=64)
-        gather_words(early_words[:], 0, S - PIECE)
-
-        late_codes = keep.tile([P, HALF * PIECE], U32, name="picked_scale", align_bytes=64)
+        late_codes = keep.tile([P, HALF * PIECE], U32, name="late_codes", align_bytes=64)
         quantise(late_codes[:], late_scale[:], late_bf[:])
         for c in range(HALF):
             multiply(HALF + c, MEMORY, late_codes[:, piece(c)], late_scale[:, piece(c)])

@@ -147,13 +147,13 @@ def tile_picked_ylmu_rnn_p_kernel(tc, x_words, x_scales, mem, w1, ar, bias, offs
 
         early_words = keep.tile([P, S - PIECE], U32, name="ar_raw", align_bytes=64)
         gather_words(early_words[:], 0, S - PIECE)
-        quantise(early_codes[:], early_scale[:], early_bf[:])
         for c in range(HALF):
+            quantise(early_codes[:, piece(c)], early_scale[:, piece(c)], early_bf[:, piece(c), :])
             multiply(c, MEMORY, early_codes[:, piece(c)], early_scale[:, piece(c)])
 
         late_codes = keep.tile([P, HALF * PIECE], U32, name="late_codes", align_bytes=64)
-        quantise(late_codes[:], late_scale[:], late_bf[:])
         for c in range(HALF):
+            quantise(late_codes[:, piece(c)], late_scale[:, piece(c)], late_bf[:, piece(c), :])
             multiply(HALF + c, MEMORY, late_codes[:, piece(c)], late_scale[:, piece(c)])
 
         quantise(w_code[INPUT][:], w_scale[INPUT][:], w_bf[INPUT][:])

@@ -27,9 +27,10 @@ LIST_ROWS = 16
 RUN = 4
 PIECE = 128
 PIECES = S // PIECE
-HALF = PIECES // 2
-JOIN_CUTS = ((0, HALF * PIECE), (HALF * PIECE, S))
+HALF = S // 2
 MEMORY, INPUT = 0, 1
+SPLIT = S - PIECE
+WORD_CUTS = ((0, HALF), (HALF, S - PIECE), (S - PIECE, S))
 
 
 def tile_picked_ylmu_rnn_p_kernel(tc, x_words, x_scales, mem, w1, ar, bias, offs, slot, out):
@@ -42,10 +43,23 @@ def tile_picked_ylmu_rnn_p_kernel(tc, x_words, x_scales, mem, w1, ar, bias, offs
         slot_sb = keep.tile([P, S // LIST_ROWS], U16, name="slot_sb")
         scale_table = keep.tile([P, T], U8, name="scale_table", align_bytes=64)
         word_table = keep.tile([P, T], I32, name="word_table", align_bytes=64)
-        mem_planes = [keep.tile([P, U], F32, name="mem_plane%d" % t, align_bytes=64) for t in range(PACK)]
-        ar_raw = keep.tile([P, PACK, N], F32, name="ar_raw", align_bytes=64)
-        w1_raw = keep.tile([P, PACK, N], F32, name="w1_raw", align_bytes=64)
+        planes = [keep.tile([P, U], F32, name="plane%d" % t, align_bytes=64) for t in range(PACK)]
+        w_raw = [keep.tile([P, PACK, N], F32, name="w_raw%d" % i, align_bytes=64) for i in (MEMORY, INPUT)]
         bias_sb = keep.tile([P, 1], F32, name="bias_sb")
+        picked_scale = keep.tile([P, S], U8, name="picked_scale", align_bytes=64)
+        x_scale = keep.tile([P, S], U8, name="x_scale", align_bytes=64)
+        h_pairs = keep.tile([P, PAIRS * SPLIT * PAIRS], BF16, name="h_pairs", align_bytes=64)
+        pair_values = h_pairs[:].rearrange("p (u j e) -> p u j e", u=PAIRS, e=PAIRS)
+        h_rows = keep.tile([P, PACK, S - SPLIT], BF16, name="h_rows", align_bytes=64)
+        early_bf = keep.tile([P, SPLIT, PACK], BF16, name="early_bf", align_bytes=64)
+        late_bf = keep.tile([P, S - SPLIT, PACK], BF16, name="late_bf", align_bytes=64)
+        h_code = [keep.tile([P, PIECE], U32, name="h_code%d" % c, align_bytes=64) for c in range(PIECES)]
+        h_scale = [keep.tile([P, PIECE], U8, name="h_scale%d" % c, align_bytes=64) for c in range(PIECES)]
+        w_bf = [keep.tile([P, N, PACK], BF16, name="w_bf%d" % i, align_bytes=64) for i in (MEMORY, INPUT)]
+        w_code = [keep.tile([P, N], U32, name="w_code%d" % i, align_bytes=64) for i in (MEMORY, INPUT)]
+        w_scale = [keep.tile([P, N], U8, name="w_scale%d" % i, align_bytes=64) for i in (MEMORY, INPUT)]
+        acc = [psum.tile([N, PIECE], F32, name="acc%d" % c) for c in range(PIECES)]
+        result = [keep.tile([N, PIECE], F32, name="result%d" % c) for c in range(PIECES)]
 
         def entries(list_tile, a, b):
             return list_tile[:, a // LIST_ROWS : b // LIST_ROWS]
@@ -53,56 +67,10 @@ def tile_picked_ylmu_rnn_p_kernel(tc, x_words, x_scales, mem, w1, ar, bias, offs
         def piece(c):
             return slice(c * PIECE, (c + 1) * PIECE)
 
-        nc.vector.memset(scale_table[0:FIRST_ROW, :].bitcast(I32), 0)
-
-        mem_view = mem.rearrange("(p t) u -> p t u", t=PACK)
-        nc.scalar.dma_start(scale_table[FIRST_ROW:P, :].bitcast(I32), x_scales[0].bitcast(I32))
-        nc.sync.dma_start(offs_sb[:], offs)
-        for t in range(PACK):
-            nc.sync.dma_start(mem_planes[t][:], mem_view[:, t, :])
-            if t == 0:
-                nc.sync.dma_start(slot_sb[:], slot)
-        nc.sync.dma_start(ar_raw[:], ar.rearrange("(p t) n -> p t n", t=PACK))
-        nc.sync.dma_start(word_table[:], x_words[0].rearrange("p c t -> p (c t)").bitcast(I32))
-
-        x_scale = keep.tile([P, S], U8, name="x_scale", align_bytes=64)
-        picked_scale = keep.tile([P, S], U8, name="picked_scale", align_bytes=64)
-        nc.vector.memset(x_scale[:].bitcast(I32), 0)
-
-        h_pairs = keep.tile([P, PAIRS * S * PAIRS], BF16, name="h_pairs", align_bytes=64)
-        pair_values = h_pairs[:].rearrange("p (u j e) -> p u j e", u=PAIRS, e=PAIRS)
-        pair_words = h_pairs[:].bitcast(U32).rearrange("p (u j) -> p u j", u=PAIRS)
-        first_planes = keep.tile([P, PAIRS, S], BF16, name="first_planes", align_bytes=64)
-        early_bf = keep.tile([P, HALF * PIECE, PACK], BF16, name="early_bf", align_bytes=64)
-        early_scale = keep.tile([P, HALF * PIECE], U8, name="early_scale", align_bytes=64)
-        early_codes = keep.tile([P, HALF * PIECE], U32, name="early_codes", align_bytes=64)
-        late_bf = keep.tile([P, HALF * PIECE, PACK], BF16, name="late_bf", align_bytes=64)
-        late_scale = keep.tile([P, HALF * PIECE], U8, name="late_scale", align_bytes=64)
-        w_raw = (ar_raw, w1_raw)
-        w_bf = [keep.tile([P, N, PACK], BF16, name="w_bf%d" % i, align_bytes=64) for i in (MEMORY, INPUT)]
-        w_code = [keep.tile([P, N], U32, name="w_code%d" % i, align_bytes=64) for i in (MEMORY, INPUT)]
-        w_scale = [keep.tile([P, N], U8, name="w_scale%d" % i, align_bytes=64) for i in (MEMORY, INPUT)]
-        acc = [psum.tile([N, PIECE], F32, name="acc%d" % c) for c in range(PIECES)]
-        result = [keep.tile([N, PIECE], F32, name="result%d" % c) for c in range(PIECES)]
-
-        def gather_plane(target, t, a, b):
-            nc.vector.tensor_copy(target[:, a:b], mem_planes[t][:].indirect(entries(slot_sb, a, b)))
-
-        def gather_words(words, a, b):
-            nc.vector.tensor_copy(words, word_table[:].bitcast(U32).indirect(entries(offs_sb, a, b)))
-
-        def join_pairs(values, a, b):
-            joined = values.rearrange("p j t -> p (j t)").bitcast(U32)
-            nc.scalar.copy(
-                joined.rearrange("p (g i u) -> p g u i", i=RUN, u=PAIRS),
-                pair_words[:, :, a:b].rearrange("p u (g i) -> p g u i", i=RUN),
-            )
-
-        def round_weight(i):
-            nc.scalar.activation(
-                w_bf[i][:].rearrange("p (g i) t -> p g t i", i=RUN),
-                w_raw[i][:].rearrange("p t (g i) -> p g t i", i=RUN),
-                COPY,
+        def by_runs(values, rows):
+            return (
+                values[:].rearrange("p (g i) t -> p g t i", i=RUN),
+                rows[:].rearrange("p t (g i) -> p g t i", i=RUN),
             )
 
         def quantise(code, scale, values):
@@ -119,8 +87,21 @@ def tile_picked_ylmu_rnn_p_kernel(tc, x_words, x_scales, mem, w1, ar, bias, offs
                 stop=(i == INPUT),
             )
 
+        nc.vector.memset(scale_table[0:FIRST_ROW, :].bitcast(I32), 0)
+        nc.vector.memset(x_scale[:].bitcast(I32), 0)
+
+        mem_view = mem.rearrange("(p t) u -> p t u", t=PACK)
+        nc.scalar.dma_start(scale_table[FIRST_ROW:P, :].bitcast(I32), x_scales[0].bitcast(I32))
+        nc.sync.dma_start(offs_sb[:], offs)
+        for t in range(PACK):
+            nc.sync.dma_start(planes[t][:], mem_view[:, t, :])
+            if t == 0:
+                nc.sync.dma_start(slot_sb[:], slot)
+        nc.sync.dma_start(w_raw[MEMORY][:], ar.rearrange("(p t) n -> p t n", t=PACK))
+        nc.sync.dma_start(w_raw[INPUT][:], w1.rearrange("(p t) n -> p t n", t=PACK))
+        nc.sync.dma_start(word_table[:], x_words[0].rearrange("p c t -> p (c t)").bitcast(I32))
+
         nc.vector.tensor_copy(picked_scale[:], scale_table[:].indirect(offs_sb[:]))
-        nc.sync.dma_start(w1_raw[:], w1.rearrange("(p t) n -> p t n", t=PACK))
         for q in range(QUADRANTS):
             nc.sync.dma_start(
                 x_scale[QUADRANT * q : QUADRANT * q + ROWS_A_QUADRANT, :].bitcast(I32),
@@ -128,40 +109,33 @@ def tile_picked_ylmu_rnn_p_kernel(tc, x_words, x_scales, mem, w1, ar, bias, offs
             )
         nc.sync.dma_start(bias_sb[:], bias)
 
-        for e in range(PAIRS):
-            gather_plane(first_planes[:, e, :], e, 0, S)
-        nc.scalar.copy(
-            pair_values[:, 0, :, :].rearrange("p (g i) e -> p g e i", i=RUN),
-            first_planes[:].rearrange("p e (g i) -> p g e i", i=RUN),
+        for t in range(PACK):
+            nc.vector.tensor_copy(
+                pair_values[:, t // PAIRS, :, t % PAIRS], planes[t][:].indirect(entries(slot_sb, 0, SPLIT))
+            )
+            nc.scalar.activation(h_rows[:, t, :], planes[t][:].indirect(entries(slot_sb, SPLIT, S)), COPY)
+        nc.scalar.copy(*by_runs(late_bf, h_rows))
+        for i in (MEMORY, INPUT):
+            nc.scalar.activation(*by_runs(w_bf[i], w_raw[i]), COPY)
+
+        joined = early_bf[:].rearrange("p j t -> p (j t)").bitcast(I32)
+        nc.vector.tensor_copy(
+            joined.rearrange("p (g i u) -> p g u i", i=RUN, u=PAIRS),
+            h_pairs[:].bitcast(I32).rearrange("p (u g i) -> p g u i", u=PAIRS, i=RUN),
         )
-        gather_plane(pair_values[:, 1, :, 0], PACK - 2, 0, S)
-        for a, b in JOIN_CUTS:
-            gather_plane(pair_values[:, 1, :, 1], PACK - 1, a, b)
-
-        round_weight(MEMORY)
-        join_pairs(early_bf[:], *JOIN_CUTS[0])
-        join_pairs(late_bf[:], *JOIN_CUTS[1])
-        round_weight(INPUT)
-
+        last = PIECES - 1
+        quantise(h_code[last][:], h_scale[last][:], late_bf[:])
         quantise(w_code[MEMORY][:], w_scale[MEMORY][:], w_bf[MEMORY][:])
-
-        early_words = keep.tile([P, S - PIECE], U32, name="ar_raw", align_bytes=64)
-        gather_words(early_words[:], 0, S - PIECE)
-        for c in range(HALF):
-            quantise(early_codes[:, piece(c)], early_scale[:, piece(c)], early_bf[:, piece(c), :])
-            multiply(c, MEMORY, early_codes[:, piece(c)], early_scale[:, piece(c)])
-
-        late_codes = keep.tile([P, HALF * PIECE], U32, name="late_codes", align_bytes=64)
-        for c in range(HALF):
-            quantise(late_codes[:, piece(c)], late_scale[:, piece(c)], late_bf[:, piece(c), :])
-            multiply(HALF + c, MEMORY, late_codes[:, piece(c)], late_scale[:, piece(c)])
-
+        for c in range(last):
+            quantise(h_code[c][:], h_scale[c][:], early_bf[:, piece(c), :])
         quantise(w_code[INPUT][:], w_scale[INPUT][:], w_bf[INPUT][:])
-        late_words = keep.tile([P, PIECE], U32, name="w1_raw", align_bytes=64)
-        gather_words(late_words[:], S - PIECE, S)
-
         for c in range(PIECES):
-            words = early_words[:, piece(c)] if c < PIECES - 1 else late_words[:]
-            multiply(c, INPUT, words, x_scale[:, piece(c)])
-            nc.scalar.activation(result[c][:], acc[c][:], TANH, bias=bias_sb[:])
-            nc.sync.dma_start(out[:, piece(c)], result[c][:])
+            multiply(c, MEMORY, h_code[c][:], h_scale[c][:])
+
+        words = keep.tile([P, S], U32, name="w_raw1", align_bytes=64)
+        for a, b in WORD_CUTS:
+            nc.vector.tensor_copy(words[:, a:b], word_table[:].bitcast(U32).indirect(entries(offs_sb, a, b)))
+            for c in range(a // PIECE, b // PIECE):
+                multiply(c, INPUT, words[:, piece(c)], x_scale[:, piece(c)])
+                nc.scalar.activation(result[c][:], acc[c][:], TANH, bias=bias_sb[:])
+                nc.sync.dma_start(out[:, piece(c)], result[c][:])

@@ -17,7 +17,6 @@ TANH = mybir.ActivationFunctionType.Tanh
 
 P = 128
 PACK = 4
-PAIRS = 2
 QUADRANTS = 4
 QUADRANT = P // QUADRANTS
 SCALE_ROWS = K // 32
@@ -29,7 +28,7 @@ PIECE = 128
 PIECES = S // PIECE
 HALF = S // 2
 MEMORY, INPUT = 0, 1
-SPLIT = S - PIECE
+SPLIT = 352
 WORD_CUTS = ((0, HALF), (HALF, S - PIECE), (S - PIECE, S))
 
 
@@ -48,11 +47,8 @@ def tile_picked_ylmu_rnn_p_kernel(tc, x_words, x_scales, mem, w1, ar, bias, offs
         bias_sb = keep.tile([P, 1], F32, name="bias_sb")
         picked_scale = keep.tile([P, S], U8, name="picked_scale", align_bytes=64)
         x_scale = keep.tile([P, S], U8, name="x_scale", align_bytes=64)
-        h_pairs = keep.tile([P, PAIRS * SPLIT * PAIRS], BF16, name="h_pairs", align_bytes=64)
-        pair_values = h_pairs[:].rearrange("p (u j e) -> p u j e", u=PAIRS, e=PAIRS)
         h_rows = keep.tile([P, PACK, S - SPLIT], BF16, name="h_rows", align_bytes=64)
-        early_bf = keep.tile([P, SPLIT, PACK], BF16, name="early_bf", align_bytes=64)
-        late_bf = keep.tile([P, S - SPLIT, PACK], BF16, name="late_bf", align_bytes=64)
+        h_bf = keep.tile([P, S, PACK], BF16, name="h_bf", align_bytes=64)
         h_code = [keep.tile([P, PIECE], U32, name="h_code%d" % c, align_bytes=64) for c in range(PIECES)]
         h_scale = [keep.tile([P, PIECE], U8, name="h_scale%d" % c, align_bytes=64) for c in range(PIECES)]
         w_bf = [keep.tile([P, N, PACK], BF16, name="w_bf%d" % i, align_bytes=64) for i in (MEMORY, INPUT)]
@@ -69,8 +65,8 @@ def tile_picked_ylmu_rnn_p_kernel(tc, x_words, x_scales, mem, w1, ar, bias, offs
 
         def by_runs(values, rows):
             return (
-                values[:].rearrange("p (g i) t -> p g t i", i=RUN),
-                rows[:].rearrange("p t (g i) -> p g t i", i=RUN),
+                values.rearrange("p (g i) t -> p g t i", i=RUN),
+                rows.rearrange("p t (g i) -> p g t i", i=RUN),
             )
 
         def quantise(code, scale, values):
@@ -110,24 +106,16 @@ def tile_picked_ylmu_rnn_p_kernel(tc, x_words, x_scales, mem, w1, ar, bias, offs
         nc.sync.dma_start(bias_sb[:], bias)
 
         for t in range(PACK):
-            nc.vector.tensor_copy(
-                pair_values[:, t // PAIRS, :, t % PAIRS], planes[t][:].indirect(entries(slot_sb, 0, SPLIT))
-            )
+            nc.vector.tensor_copy(h_bf[:, 0:SPLIT, t], planes[t][:].indirect(entries(slot_sb, 0, SPLIT)))
             nc.scalar.activation(h_rows[:, t, :], planes[t][:].indirect(entries(slot_sb, SPLIT, S)), COPY)
-        nc.scalar.copy(*by_runs(late_bf, h_rows))
-        for i in (MEMORY, INPUT):
-            nc.scalar.activation(*by_runs(w_bf[i], w_raw[i]), COPY)
+        nc.scalar.copy(*by_runs(h_bf[:, SPLIT:S, :], h_rows[:]))
+        nc.scalar.activation(*by_runs(w_bf[MEMORY][:, N // 2 : N, :], w_raw[MEMORY][:, :, N // 2 : N]), COPY)
+        nc.scalar.activation(*by_runs(w_bf[INPUT][:], w_raw[INPUT][:]), COPY)
 
-        joined = early_bf[:].rearrange("p j t -> p (j t)").bitcast(I32)
-        nc.vector.tensor_copy(
-            joined.rearrange("p (g i u) -> p g u i", i=RUN, u=PAIRS),
-            h_pairs[:].bitcast(I32).rearrange("p (u g i) -> p g u i", u=PAIRS, i=RUN),
-        )
-        last = PIECES - 1
-        quantise(h_code[last][:], h_scale[last][:], late_bf[:])
+        nc.vector.tensor_copy(*by_runs(w_bf[MEMORY][:, 0 : N // 2, :], w_raw[MEMORY][:, :, 0 : N // 2]))
+        for c in range(PIECES):
+            quantise(h_code[c][:], h_scale[c][:], h_bf[:, piece(c), :])
         quantise(w_code[MEMORY][:], w_scale[MEMORY][:], w_bf[MEMORY][:])
-        for c in range(last):
-            quantise(h_code[c][:], h_scale[c][:], early_bf[:, piece(c), :])
         quantise(w_code[INPUT][:], w_scale[INPUT][:], w_bf[INPUT][:])
         for c in range(PIECES):
             multiply(c, MEMORY, h_code[c][:], h_scale[c][:])

@@ -109,10 +109,16 @@ def tile_picked_ylmu_rnn_p_kernel(tc, x_words, x_scales, mem, w1, ar, bias, offs
             nc.vector.tensor_copy(h_bf[:, 0:SPLIT, t], planes[t][:].indirect(entries(slot_sb, 0, SPLIT)))
             nc.scalar.activation(h_rows[:, t, :], planes[t][:].indirect(entries(slot_sb, SPLIT, S)), COPY)
         nc.scalar.copy(*by_runs(h_bf[:, SPLIT:S, :], h_rows[:]))
-        nc.scalar.activation(*by_runs(w_bf[MEMORY][:, N // 2 : N, :], w_raw[MEMORY][:, :, N // 2 : N]), COPY)
         nc.scalar.activation(*by_runs(w_bf[INPUT][:], w_raw[INPUT][:]), COPY)
 
-        nc.vector.tensor_copy(*by_runs(w_bf[MEMORY][:, 0 : N // 2, :], w_raw[MEMORY][:, :, 0 : N // 2]))
+        nc.gpsimd.tensor_scalar(
+            w_bf[MEMORY][:],
+            w_raw[MEMORY][:].rearrange("p t n -> p n t"),
+            1.0,
+            0.0,
+            mybir.AluOpType.mult,
+            mybir.AluOpType.add,
+        )
         for c in range(PIECES):
             quantise(h_code[c][:], h_scale[c][:], h_bf[:, piece(c), :])
         quantise(w_code[MEMORY][:], w_scale[MEMORY][:], w_bf[MEMORY][:])

@@ -41,10 +41,8 @@ def tile_picked_ylmu_rnn_p_kernel(tc, x_words, x_scales, mem, w1, ar, bias, offs
         offs_sb = keep.tile([P, S // LIST_ROWS], U16, name="offs_sb")
         slot_sb = keep.tile([P, S // LIST_ROWS], U16, name="slot_sb")
         scale_table = keep.tile([P, T], U8, name="scale_table", align_bytes=64)
-        word_table = keep.tile([P, T], I32, name="word_table", align_bytes=64)
         planes = [keep.tile([P, U], F32, name="plane%d" % t, align_bytes=64) for t in range(PACK)]
         w_raw = [keep.tile([P, PACK, N], F32, name="w_raw%d" % i, align_bytes=64) for i in (MEMORY, INPUT)]
-        bias_sb = keep.tile([P, 1], F32, name="bias_sb")
         picked_scale = keep.tile([P, S], U8, name="picked_scale", align_bytes=64)
         x_scale = keep.tile([P, S], U8, name="x_scale", align_bytes=64)
         h_rows = keep.tile([P, PACK, S - SPLIT], BF16, name="h_rows", align_bytes=64)
@@ -95,14 +93,16 @@ def tile_picked_ylmu_rnn_p_kernel(tc, x_words, x_scales, mem, w1, ar, bias, offs
                 nc.sync.dma_start(slot_sb[:], slot)
         nc.sync.dma_start(w_raw[MEMORY][:], ar.rearrange("(p t) n -> p t n", t=PACK))
         nc.sync.dma_start(w_raw[INPUT][:], w1.rearrange("(p t) n -> p t n", t=PACK))
-        nc.sync.dma_start(word_table[:], x_words[0].rearrange("p c t -> p (c t)").bitcast(I32))
-
         nc.vector.tensor_copy(picked_scale[:], scale_table[:].indirect(offs_sb[:]))
         for q in range(QUADRANTS):
             nc.sync.dma_start(
                 x_scale[QUADRANT * q : QUADRANT * q + ROWS_A_QUADRANT, :].bitcast(I32),
                 picked_scale[FIRST_ROW + ROWS_A_QUADRANT * q : FIRST_ROW + ROWS_A_QUADRANT * (q + 1), :].bitcast(I32),
             )
+        word_table = keep.tile([P, T], I32, name="scale_table", align_bytes=64)
+        nc.sync.dma_start(word_table[:], x_words[0].rearrange("p c t -> p (c t)").bitcast(I32))
+
+        bias_sb = keep.tile([P, 1], F32, name="picked_scale", align_bytes=64)
         nc.sync.dma_start(bias_sb[:], bias)
 
         for t in range(PACK):

@@ -36,11 +36,12 @@ def tile_picked_ylmu_rnn_p_kernel(tc, x_words, x_scales, mem, w1, ar, bias, offs
     nc = tc.nc
     with ExitStack() as ctx:
         keep = ctx.enter_context(tc.tile_pool(name="keep", bufs=1))
+        shared = ctx.enter_context(tc.tile_pool(name="shared", bufs=1))
         psum = ctx.enter_context(tc.psum_pool(name="psum", bufs=1))
 
         offs_sb = keep.tile([P, S // LIST_ROWS], U16, name="offs_sb")
         slot_sb = keep.tile([P, S // LIST_ROWS], U16, name="slot_sb")
-        scale_table = keep.tile([P, T], U8, name="scale_table", align_bytes=64)
+        scale_table = shared.tile([P, T], U8, name="scale_table", align_bytes=64, offset=0)
         planes = [keep.tile([P, U], F32, name="plane%d" % t, align_bytes=64) for t in range(PACK)]
         w_raw = [keep.tile([P, PACK, N], F32, name="w_raw%d" % i, align_bytes=64) for i in (MEMORY, INPUT)]
         picked_scale = keep.tile([P, S], U8, name="picked_scale", align_bytes=64)
@@ -99,10 +100,10 @@ def tile_picked_ylmu_rnn_p_kernel(tc, x_words, x_scales, mem, w1, ar, bias, offs
                 x_scale[QUADRANT * q : QUADRANT * q + ROWS_A_QUADRANT, :].bitcast(I32),
                 picked_scale[FIRST_ROW + ROWS_A_QUADRANT * q : FIRST_ROW + ROWS_A_QUADRANT * (q + 1), :].bitcast(I32),
             )
-        word_table = keep.tile([P, T], I32, name="scale_table", align_bytes=64)
+        word_table = shared.tile([P, T], I32, name="word_table", align_bytes=64, offset=64)
         nc.sync.dma_start(word_table[:], x_words[0].rearrange("p c t -> p (c t)").bitcast(I32))
 
-        bias_sb = keep.tile([P, 1], F32, name="picked_scale", align_bytes=64)
+        bias_sb = shared.tile([P, 1], F32, name="bias_sb", align_bytes=64, offset=0)
         nc.sync.dma_start(bias_sb[:], bias)
 
         for t in range(PACK):

@@ -95,10 +95,10 @@ def tile_picked_ylmu_rnn_p_kernel(tc, x_words, x_scales, mem, w1, ar, bias, offs
         nc.sync.dma_start(w_raw[MEMORY][:], ar.rearrange("(p t) n -> p t n", t=PACK))
         nc.sync.dma_start(w_raw[INPUT][:], w1.rearrange("(p t) n -> p t n", t=PACK))
         nc.vector.tensor_copy(picked_scale[:], scale_table[:].indirect(offs_sb[:]))
-        for q in range(QUADRANTS):
+        for r in range(ROWS_A_QUADRANT):
             nc.sync.dma_start(
-                x_scale[QUADRANT * q : QUADRANT * q + ROWS_A_QUADRANT, :].bitcast(I32),
-                picked_scale[FIRST_ROW + ROWS_A_QUADRANT * q : FIRST_ROW + ROWS_A_QUADRANT * (q + 1), :].bitcast(I32),
+                x_scale[r:P:QUADRANT, :].bitcast(I32),
+                picked_scale[FIRST_ROW + r : P : ROWS_A_QUADRANT, :].bitcast(I32),
             )
         word_table = shared.tile([P, T], I32, name="word_table", align_bytes=64, offset=64)
         nc.sync.dma_start(word_table[:], x_words[0].rearrange("p c t -> p (c t)").bitcast(I32))

@@ -26,10 +26,8 @@ LIST_ROWS = 16
 RUN = 4
 PIECE = 128
 PIECES = S // PIECE
-HALF = S // 2
 MEMORY, INPUT = 0, 1
 SPLIT = 352
-WORD_CUTS = ((0, HALF), (HALF, S - PIECE), (S - PIECE, S))
 
 
 def tile_picked_ylmu_rnn_p_kernel(tc, x_words, x_scales, mem, w1, ar, bias, offs, slot, out):
@@ -128,9 +126,10 @@ def tile_picked_ylmu_rnn_p_kernel(tc, x_words, x_scales, mem, w1, ar, bias, offs
             multiply(c, MEMORY, h_code[c][:], h_scale[c][:])
 
         words = keep.tile([P, S], U32, name="w_raw1", align_bytes=64)
-        for a, b in WORD_CUTS:
-            nc.vector.tensor_copy(words[:, a:b], word_table[:].bitcast(U32).indirect(entries(offs_sb, a, b)))
-            for c in range(a // PIECE, b // PIECE):
-                multiply(c, INPUT, words[:, piece(c)], x_scale[:, piece(c)])
-                nc.scalar.activation(result[c][:], acc[c][:], TANH, bias=bias_sb[:])
-                nc.sync.dma_start(out[:, piece(c)], result[c][:])
+        for c in range(PIECES):
+            nc.vector.tensor_copy(
+                words[:, piece(c)], word_table[:].bitcast(U32).indirect(entries(offs_sb, c * PIECE, (c + 1) * PIECE))
+            )
+            multiply(c, INPUT, words[:, piece(c)], x_scale[:, piece(c)])
+            nc.scalar.activation(result[c][:], acc[c][:], TANH, bias=bias_sb[:])
+            nc.sync.dma_start(out[:, piece(c)], result[c][:])

@@ -26,8 +26,9 @@ LIST_ROWS = 16
 RUN = 4
 PIECE = 128
 PIECES = S // PIECE
+HALF = S // 2
 MEMORY, INPUT = 0, 1
-SPLIT = 352
+DMA_ALIGN = 256
 
 
 def tile_picked_ylmu_rnn_p_kernel(tc, x_words, x_scales, mem, w1, ar, bias, offs, slot, out):
@@ -39,20 +40,18 @@ def tile_picked_ylmu_rnn_p_kernel(tc, x_words, x_scales, mem, w1, ar, bias, offs
 
         offs_sb = keep.tile([P, S // LIST_ROWS], U16, name="offs_sb")
         slot_sb = keep.tile([P, S // LIST_ROWS], U16, name="slot_sb")
-        scale_table = shared.tile([P, T], U8, name="scale_table", align_bytes=64, offset=0)
-        planes = [keep.tile([P, U], F32, name="plane%d" % t, align_bytes=64) for t in range(PACK)]
-        w_raw = [keep.tile([P, PACK, N], F32, name="w_raw%d" % i, align_bytes=64) for i in (MEMORY, INPUT)]
-        picked_scale = keep.tile([P, S], U8, name="picked_scale", align_bytes=64)
-        x_scale = keep.tile([P, S], U8, name="x_scale", align_bytes=64)
-        h_rows = keep.tile([P, PACK, S - SPLIT], BF16, name="h_rows", align_bytes=64)
-        h_bf = keep.tile([P, S, PACK], BF16, name="h_bf", align_bytes=64)
-        h_code = [keep.tile([P, PIECE], U32, name="h_code%d" % c, align_bytes=64) for c in range(PIECES)]
+        scale_table = shared.tile([P, T], U8, name="scale_table", align_bytes=DMA_ALIGN, offset=0)
+        planes = [keep.tile([P, U], F32, name="plane%d" % t, align_bytes=DMA_ALIGN) for t in range(PACK)]
+        w_raw = [keep.tile([P, PACK, N], F32, name="w_raw%d" % i, align_bytes=DMA_ALIGN) for i in (MEMORY, INPUT)]
+        picked_scale = keep.tile([P, S], U8, name="picked_scale", align_bytes=DMA_ALIGN)
+        x_scale = keep.tile([P, S], U8, name="x_scale", align_bytes=DMA_ALIGN)
+        h_bf = [keep.tile([P, HALF, PACK], BF16, name="h_bf%d" % e, align_bytes=64) for e in range(2)]
         h_scale = [keep.tile([P, PIECE], U8, name="h_scale%d" % c, align_bytes=64) for c in range(PIECES)]
         w_bf = [keep.tile([P, N, PACK], BF16, name="w_bf%d" % i, align_bytes=64) for i in (MEMORY, INPUT)]
         w_code = [keep.tile([P, N], U32, name="w_code%d" % i, align_bytes=64) for i in (MEMORY, INPUT)]
         w_scale = [keep.tile([P, N], U8, name="w_scale%d" % i, align_bytes=64) for i in (MEMORY, INPUT)]
         acc = [psum.tile([N, PIECE], F32, name="acc%d" % c) for c in range(PIECES)]
-        result = [keep.tile([N, PIECE], F32, name="result%d" % c) for c in range(PIECES)]
+        result = [keep.tile([N, PIECE], F32, name="result%d" % c, align_bytes=DMA_ALIGN) for c in range(PIECES)]
 
         def entries(list_tile, a, b):
             return list_tile[:, a // LIST_ROWS : b // LIST_ROWS]
@@ -83,6 +82,9 @@ def tile_picked_ylmu_rnn_p_kernel(tc, x_words, x_scales, mem, w1, ar, bias, offs
         nc.vector.memset(scale_table[0:FIRST_ROW, :].bitcast(I32), 0)
         nc.vector.memset(x_scale[:].bitcast(I32), 0)
 
+        warm = keep.tile([P, 1], F32, name="warm")
+        warm_out = keep.tile([P, 1], F32, name="warm_out")
+        nc.gpsimd.memset(warm[:], 0.0)
         mem_view = mem.rearrange("(p t) u -> p t u", t=PACK)
         nc.scalar.dma_start(scale_table[FIRST_ROW:P, :].bitcast(I32), x_scales[0].bitcast(I32))
         nc.sync.dma_start(offs_sb[:], offs)
@@ -92,40 +94,34 @@ def tile_picked_ylmu_rnn_p_kernel(tc, x_words, x_scales, mem, w1, ar, bias, offs
                 nc.sync.dma_start(slot_sb[:], slot)
         nc.sync.dma_start(w_raw[MEMORY][:], ar.rearrange("(p t) n -> p t n", t=PACK))
         nc.sync.dma_start(w_raw[INPUT][:], w1.rearrange("(p t) n -> p t n", t=PACK))
+        nc.scalar.activation(warm_out[:], warm[:], TANH)
         nc.vector.tensor_copy(picked_scale[:], scale_table[:].indirect(offs_sb[:]))
         for r in range(ROWS_A_QUADRANT):
             nc.sync.dma_start(
                 x_scale[r:P:QUADRANT, :].bitcast(I32),
                 picked_scale[FIRST_ROW + r : P : ROWS_A_QUADRANT, :].bitcast(I32),
             )
-        word_table = shared.tile([P, T], I32, name="word_table", align_bytes=64, offset=64)
+        word_table = shared.tile([P, T], I32, name="word_table", align_bytes=DMA_ALIGN, offset=DMA_ALIGN)
         nc.sync.dma_start(word_table[:], x_words[0].rearrange("p c t -> p (c t)").bitcast(I32))
 
-        bias_sb = shared.tile([P, 1], F32, name="bias_sb", align_bytes=64, offset=0)
+        bias_sb = shared.tile([P, 1], F32, name="bias_sb", align_bytes=DMA_ALIGN, offset=0)
         nc.sync.dma_start(bias_sb[:], bias)
 
         for t in range(PACK):
-            nc.vector.tensor_copy(h_bf[:, 0:SPLIT, t], planes[t][:].indirect(entries(slot_sb, 0, SPLIT)))
-            nc.scalar.activation(h_rows[:, t, :], planes[t][:].indirect(entries(slot_sb, SPLIT, S)), COPY)
-        nc.scalar.copy(*by_runs(h_bf[:, SPLIT:S, :], h_rows[:]))
+            nc.vector.tensor_copy(h_bf[0][:, :, t], planes[t][:].indirect(entries(slot_sb, 0, HALF)))
+            nc.scalar.activation(h_bf[1][:, :, t], planes[t][:].indirect(entries(slot_sb, HALF, S)), COPY)
+        nc.vector.tensor_copy(*by_runs(w_bf[MEMORY][:], w_raw[MEMORY][:]))
         nc.scalar.activation(*by_runs(w_bf[INPUT][:], w_raw[INPUT][:]), COPY)
 
-        nc.gpsimd.tensor_scalar(
-            w_bf[MEMORY][:],
-            w_raw[MEMORY][:].rearrange("p t n -> p n t"),
-            1.0,
-            0.0,
-            mybir.AluOpType.mult,
-            mybir.AluOpType.add,
-        )
-        for c in range(PIECES):
-            quantise(h_code[c][:], h_scale[c][:], h_bf[:, piece(c), :])
         quantise(w_code[MEMORY][:], w_scale[MEMORY][:], w_bf[MEMORY][:])
+        h_code = keep.tile([P, S], U32, name="w_raw0", align_bytes=DMA_ALIGN)
+        for c in range(PIECES):
+            quantise(h_code[:, piece(c)], h_scale[c][:], h_bf[c // 2][:, piece(c % 2), :])
         quantise(w_code[INPUT][:], w_scale[INPUT][:], w_bf[INPUT][:])
         for c in range(PIECES):
-            multiply(c, MEMORY, h_code[c][:], h_scale[c][:])
+            multiply(c, MEMORY, h_code[:, piece(c)], h_scale[c][:])
 
-        words = keep.tile([P, S], U32, name="w_raw1", align_bytes=64)
+        words = keep.tile([P, S], U32, name="w_raw1", align_bytes=DMA_ALIGN)
         for c in range(PIECES):
             nc.vector.tensor_copy(
                 words[:, piece(c)], word_table[:].bitcast(U32).indirect(entries(offs_sb, c * PIECE, (c + 1) * PIECE))

@@ -26,7 +26,7 @@ LIST_ROWS = 16
 RUN = 4
 PIECE = 128
 PIECES = S // PIECE
-HALF = S // 2
+SPLIT = 224
 MEMORY, INPUT = 0, 1
 DMA_ALIGN = 256
 
@@ -45,7 +45,7 @@ def tile_picked_ylmu_rnn_p_kernel(tc, x_words, x_scales, mem, w1, ar, bias, offs
         w_raw = [keep.tile([P, PACK, N], F32, name="w_raw%d" % i, align_bytes=DMA_ALIGN) for i in (MEMORY, INPUT)]
         picked_scale = keep.tile([P, S], U8, name="picked_scale", align_bytes=DMA_ALIGN)
         x_scale = keep.tile([P, S], U8, name="x_scale", align_bytes=DMA_ALIGN)
-        h_bf = [keep.tile([P, HALF, PACK], BF16, name="h_bf%d" % e, align_bytes=64) for e in range(2)]
+        h_bf = keep.tile([P, S, PACK], BF16, name="h_bf", align_bytes=64)
         h_scale = [keep.tile([P, PIECE], U8, name="h_scale%d" % c, align_bytes=64) for c in range(PIECES)]
         w_bf = [keep.tile([P, N, PACK], BF16, name="w_bf%d" % i, align_bytes=64) for i in (MEMORY, INPUT)]
         w_code = [keep.tile([P, N], U32, name="w_code%d" % i, align_bytes=64) for i in (MEMORY, INPUT)]
@@ -108,15 +108,15 @@ def tile_picked_ylmu_rnn_p_kernel(tc, x_words, x_scales, mem, w1, ar, bias, offs
         nc.sync.dma_start(bias_sb[:], bias)
 
         for t in range(PACK):
-            nc.vector.tensor_copy(h_bf[0][:, :, t], planes[t][:].indirect(entries(slot_sb, 0, HALF)))
-            nc.scalar.activation(h_bf[1][:, :, t], planes[t][:].indirect(entries(slot_sb, HALF, S)), COPY)
+            nc.vector.tensor_copy(h_bf[:, 0:SPLIT, t], planes[t][:].indirect(entries(slot_sb, 0, SPLIT)))
+            nc.scalar.activation(h_bf[:, SPLIT:S, t], planes[t][:].indirect(entries(slot_sb, SPLIT, S)), COPY)
         nc.vector.tensor_copy(*by_runs(w_bf[MEMORY][:], w_raw[MEMORY][:]))
         nc.scalar.activation(*by_runs(w_bf[INPUT][:], w_raw[INPUT][:]), COPY)
 
         quantise(w_code[MEMORY][:], w_scale[MEMORY][:], w_bf[MEMORY][:])
         h_code = keep.tile([P, S], U32, name="w_raw0", align_bytes=DMA_ALIGN)
         for c in range(PIECES):
-            quantise(h_code[:, piece(c)], h_scale[c][:], h_bf[c // 2][:, piece(c % 2), :])
+            quantise(h_code[:, piece(c)], h_scale[c][:], h_bf[:, piece(c), :])
         quantise(w_code[INPUT][:], w_scale[INPUT][:], w_bf[INPUT][:])
         for c in range(PIECES):
             multiply(c, MEMORY, h_code[:, piece(c)], h_scale[c][:])

@@ -87,11 +87,11 @@ def tile_picked_ylmu_rnn_p_kernel(tc, x_words, x_scales, mem, w1, ar, bias, offs
         nc.gpsimd.memset(warm[:], 0.0)
         mem_view = mem.rearrange("(p t) u -> p t u", t=PACK)
         nc.scalar.dma_start(scale_table[FIRST_ROW:P, :].bitcast(I32), x_scales[0].bitcast(I32))
-        nc.sync.dma_start(offs_sb[:], offs)
         for t in range(PACK):
             nc.sync.dma_start(planes[t][:], mem_view[:, t, :])
             if t == 0:
                 nc.sync.dma_start(slot_sb[:], slot)
+                nc.sync.dma_start(offs_sb[:], offs)
         nc.sync.dma_start(w_raw[MEMORY][:], ar.rearrange("(p t) n -> p t n", t=PACK))
         nc.sync.dma_start(w_raw[INPUT][:], w1.rearrange("(p t) n -> p t n", t=PACK))
         nc.scalar.activation(warm_out[:], warm[:], TANH)

@@ -109,7 +109,9 @@ def tile_picked_ylmu_rnn_p_kernel(tc, x_words, x_scales, mem, w1, ar, bias, offs
 
         for t in range(PACK):
             nc.vector.tensor_copy(h_bf[:, 0:SPLIT, t], planes[t][:].indirect(entries(slot_sb, 0, SPLIT)))
-            nc.scalar.activation(h_bf[:, SPLIT:S, t], planes[t][:].indirect(entries(slot_sb, SPLIT, S)), COPY)
+            cuts = (SPLIT, S - PIECE, S) if t == PACK - 1 else (SPLIT, S)
+            for a, b in zip(cuts, cuts[1:]):
+                nc.scalar.activation(h_bf[:, a:b, t], planes[t][:].indirect(entries(slot_sb, a, b)), COPY)
         nc.vector.tensor_copy(*by_runs(w_bf[MEMORY][:], w_raw[MEMORY][:]))
         nc.scalar.activation(*by_runs(w_bf[INPUT][:], w_raw[INPUT][:]), COPY)
 

from contextlib import ExitStack

import concourse.mybir as mybir

K, T, S, H, N, U = 512, 1024, 512, 512, 128, 1024
FLOPS = 2 * (K + H) * N * S

F32 = mybir.dt.float32
BF16 = mybir.dt.bfloat16
I32 = mybir.dt.int32
U32 = mybir.dt.uint32
U16 = mybir.dt.uint16
U8 = mybir.dt.uint8
FP8X4 = mybir.dt.float8_e4m3fn_x4
COPY = mybir.ActivationFunctionType.Copy
TANH = mybir.ActivationFunctionType.Tanh

P = 128
PACK = 4
QUADRANTS = 4
QUADRANT = P // QUADRANTS
SCALE_ROWS = K // 32
ROWS_A_QUADRANT = SCALE_ROWS // QUADRANTS
FIRST_ROW = P - SCALE_ROWS
LIST_ROWS = 16
RUN = 4
PIECE = 128
PIECES = S // PIECE
SPLIT = 224
MEMORY, INPUT = 0, 1
DMA_ALIGN = 256


def tile_picked_ylmu_rnn_p_kernel(tc, x_words, x_scales, mem, w1, ar, bias, offs, slot, out):
    nc = tc.nc
    with ExitStack() as ctx:
        keep = ctx.enter_context(tc.tile_pool(name="keep", bufs=1))
        shared = ctx.enter_context(tc.tile_pool(name="shared", bufs=1))
        psum = ctx.enter_context(tc.psum_pool(name="psum", bufs=1))

        offs_sb = keep.tile([P, S // LIST_ROWS], U16, name="offs_sb")
        slot_sb = keep.tile([P, S // LIST_ROWS], U16, name="slot_sb")
        scale_table = shared.tile([P, T], U8, name="scale_table", align_bytes=DMA_ALIGN, offset=0)
        planes = [keep.tile([P, U], F32, name="plane%d" % t, align_bytes=DMA_ALIGN) for t in range(PACK)]
        w_raw = [keep.tile([P, PACK, N], F32, name="w_raw%d" % i, align_bytes=DMA_ALIGN) for i in (MEMORY, INPUT)]
        picked_scale = keep.tile([P, S], U8, name="picked_scale", align_bytes=DMA_ALIGN)
        x_scale = keep.tile([P, S], U8, name="x_scale", align_bytes=DMA_ALIGN)
        h_bf = keep.tile([P, S, PACK], BF16, name="h_bf", align_bytes=64)
        h_scale = [keep.tile([P, PIECE], U8, name="h_scale%d" % c, align_bytes=64) for c in range(PIECES)]
        w_bf = [keep.tile([P, N, PACK], BF16, name="w_bf%d" % i, align_bytes=64) for i in (MEMORY, INPUT)]
        w_code = [keep.tile([P, N], U32, name="w_code%d" % i, align_bytes=64) for i in (MEMORY, INPUT)]
        w_scale = [keep.tile([P, N], U8, name="w_scale%d" % i, align_bytes=64) for i in (MEMORY, INPUT)]
        acc = [psum.tile([N, PIECE], F32, name="acc%d" % c) for c in range(PIECES)]
        result = [keep.tile([N, PIECE], F32, name="result%d" % c, align_bytes=DMA_ALIGN) for c in range(PIECES)]

        def entries(list_tile, a, b):
            return list_tile[:, a // LIST_ROWS : b // LIST_ROWS]

        def piece(c):
            return slice(c * PIECE, (c + 1) * PIECE)

        def by_runs(values, rows):
            return (
                values.rearrange("p (g i) t -> p g t i", i=RUN),
                rows.rearrange("p t (g i) -> p g t i", i=RUN),
            )

        def quantise(code, scale, values):
            nc.vector.quantize_mx(out=code.bitcast(FP8X4), scales=scale, in_=values.rearrange("p c t -> p (c t)"))

        def multiply(c, i, moving, moving_scale):
            nc.tensor.matmul_mx(
                out=acc[c][:],
                lhsT=w_code[i][:].bitcast(FP8X4),
                lhsT_scale=w_scale[i][:],
                rhs=moving.bitcast(FP8X4),
                rhs_scale=moving_scale,
                start=(i == MEMORY),
                stop=(i == INPUT),
            )

        nc.vector.memset(scale_table[0:FIRST_ROW, :].bitcast(I32), 0)
        nc.vector.memset(x_scale[:].bitcast(I32), 0)

        warm = keep.tile([P, 1], F32, name="warm")
        warm_out = keep.tile([P, 1], F32, name="warm_out")
        nc.gpsimd.memset(warm[:], 0.0)
        mem_view = mem.rearrange("(p t) u -> p t u", t=PACK)
        nc.scalar.dma_start(scale_table[FIRST_ROW:P, :].bitcast(I32), x_scales[0].bitcast(I32))
        for t in range(PACK):
            nc.sync.dma_start(planes[t][:], mem_view[:, t, :])
            if t == 0:
                nc.sync.dma_start(slot_sb[:], slot)
                nc.sync.dma_start(offs_sb[:], offs)
        nc.sync.dma_start(w_raw[MEMORY][:], ar.rearrange("(p t) n -> p t n", t=PACK))
        nc.sync.dma_start(w_raw[INPUT][:], w1.rearrange("(p t) n -> p t n", t=PACK))
        nc.scalar.activation(warm_out[:], warm[:], TANH)
        nc.vector.tensor_copy(picked_scale[:], scale_table[:].indirect(offs_sb[:]))
        for r in range(ROWS_A_QUADRANT):
            nc.sync.dma_start(
                x_scale[r:P:QUADRANT, :].bitcast(I32),
                picked_scale[FIRST_ROW + r : P : ROWS_A_QUADRANT, :].bitcast(I32),
            )
        word_table = shared.tile([P, T], I32, name="word_table", align_bytes=DMA_ALIGN, offset=DMA_ALIGN)
        nc.sync.dma_start(word_table[:], x_words[0].rearrange("p c t -> p (c t)").bitcast(I32))

        bias_sb = shared.tile([P, 1], F32, name="bias_sb", align_bytes=DMA_ALIGN, offset=0)
        nc.sync.dma_start(bias_sb[:], bias)

        for t in range(PACK):
            nc.vector.tensor_copy(h_bf[:, 0:SPLIT, t], planes[t][:].indirect(entries(slot_sb, 0, SPLIT)))
            cuts = (SPLIT, S - PIECE, S) if t == PACK - 1 else (SPLIT, S)
            for a, b in zip(cuts, cuts[1:]):
                nc.scalar.activation(h_bf[:, a:b, t], planes[t][:].indirect(entries(slot_sb, a, b)), COPY)
        nc.vector.tensor_copy(*by_runs(w_bf[MEMORY][:], w_raw[MEMORY][:]))
        nc.scalar.activation(*by_runs(w_bf[INPUT][:], w_raw[INPUT][:]), COPY)

        quantise(w_code[MEMORY][:], w_scale[MEMORY][:], w_bf[MEMORY][:])
        h_code = keep.tile([P, S], U32, name="w_raw0", align_bytes=DMA_ALIGN)
        for c in range(PIECES):
            quantise(h_code[:, piece(c)], h_scale[c][:], h_bf[:, piece(c), :])
        quantise(w_code[INPUT][:], w_scale[INPUT][:], w_bf[INPUT][:])
        for c in range(PIECES):
            multiply(c, MEMORY, h_code[:, piece(c)], h_scale[c][:])

        words = keep.tile([P, S], U32, name="w_raw1", align_bytes=DMA_ALIGN)
        for c in range(PIECES):
            nc.vector.tensor_copy(
                words[:, piece(c)], word_table[:].bitcast(U32).indirect(entries(offs_sb, c * PIECE, (c + 1) * PIECE))
            )
            multiply(c, INPUT, words[:, piece(c)], x_scale[:, piece(c)])
            nc.scalar.activation(result[c][:], acc[c][:], TANH, bias=bias_sb[:])
            nc.sync.dma_start(out[:, piece(c)], result[c][:])
